import numpy as np
import ml_dtypes


def mxq(x, axis, fmt="e4m3"):
    dtype, down = {"e4m3": (ml_dtypes.float8_e4m3fn, 7), "e5m2": (ml_dtypes.float8_e5m2, 14)}[fmt]
    v = np.moveaxis(np.asarray(x, np.float32).astype(ml_dtypes.bfloat16).astype(np.float64), axis, -1)
    blocks = v.reshape(v.shape[:-1] + (-1, 32))
    amax = np.abs(blocks).max(-1, keepdims=True)
    byte = np.maximum(np.where(amax > 0, np.frexp(amax)[1] - 1 + 127, 0) - down, 1)
    scale = np.exp2(byte - 127.0)
    codes = (blocks / scale).astype(np.float32).astype(dtype).astype(np.float64)
    return np.moveaxis((codes * scale).reshape(v.shape), -1, axis)


WIDE = False


def mx_kscale(k):
    if not WIDE:
        return np.ones(k)
    levels = np.array([10, -10, 5, -5, 0])
    if k % 512:
        return np.exp2(np.random.permutation(np.resize(levels, k // 32))).repeat(32)
    a = np.empty((k // 512, 16))
    for p in range(k // 512):
        a[p, :8] = np.random.permutation(np.resize(levels, 8))
        for g in range(8):
            far = levels[np.abs(levels - a[p, g]) >= 10]
            a[p, g + 8] = far[np.random.randint(len(far))]
    return np.exp2(a.ravel()).repeat(32)


def f64(x):
    return np.asarray(x).astype(np.float64)


def striped(idx):
    return np.tile(np.asarray(idx).reshape(-1, 16).T, (8, 1)).astype(np.uint16)


def unstriped(offs):
    return offs[:16].T.reshape(-1).astype(np.int64)


E2M1 = np.array([0.0, 0.5, 1.0, 1.5, 2.0, 3.0, 4.0, 6.0, -0.0, -0.5, -1.0, -1.5, -2.0, -3.0, -4.0, -6.0])


def pack_weight(w, fmt):
    k, n = w.shape
    w = f64(np.asarray(w, np.float32).astype(ml_dtypes.bfloat16)).reshape(k // 32, 32, n)
    amax = np.abs(w).max(1)
    if fmt == "e4m3":
        byte = np.frexp(amax)[1] - 1 + 127 - 7
    else:
        mant, ex = np.frexp(amax / 6.0)
        byte = np.where(mant > 0.5, ex, ex - 1) + 127
    byte = np.clip(np.where(amax > 0, byte, 1), 1, 254)
    scaled = (w * np.exp2(127.0 - byte)[:, None, :]).reshape(k, n).astype(np.float32)
    by_word = np.ascontiguousarray(scaled.reshape(k // 512, 128, 4, n).transpose(0, 1, 3, 2))
    if fmt == "e4m3":
        words = by_word.astype(ml_dtypes.float8_e4m3fn).view(np.uint8)
    else:
        c = by_word.astype(ml_dtypes.float4_e2m1fn).view(np.uint8) & 0xF
        words = (c[..., 0::2] | (c[..., 1::2] << 4)).reshape(k // 512, 128, 2 * n)
    return np.ascontiguousarray(words), np.ascontiguousarray(byte.astype(np.uint8).reshape(k // 512, 16, n))


def unpack_weight(words, scales, fmt):
    g, _, n = scales.shape
    words = np.ascontiguousarray(words).reshape(g, 128, n, -1)
    if fmt == "e4m3":
        vals = words.view(ml_dtypes.float8_e4m3fn).astype(np.float64)
    else:
        nib = np.empty((g, 128, n, 4), np.uint8)
        nib[..., 0::2] = words & 0xF
        nib[..., 1::2] = words >> 4
        vals = E2M1[nib]
    vals = vals * np.repeat(np.exp2(scales.astype(np.float64) - 127.0), 8, axis=1)[..., None]
    return vals.transpose(0, 1, 3, 2).reshape(g * 512, n)


def bf(x):
    return np.asarray(x, np.float32).astype(ml_dtypes.bfloat16)


def planes(Y):
    r, m = Y.shape
    b = f64(bf(Y)).reshape(r // 32, 32, m)
    amax = np.abs(b).max(1)
    byte = np.clip(np.where(amax > 0, np.frexp(amax)[1] - 1 + 127 - 7, 1), 1, 254)
    codes = (b * np.exp2(127.0 - byte)[:, None, :]).reshape(r, m).astype(np.float32).astype(ml_dtypes.float8_e4m3fn).view(np.uint8)
    words = codes.reshape(r // 512, 128, 4, m).transpose(0, 1, 3, 2)
    return np.ascontiguousarray(words), np.ascontiguousarray(byte.astype(np.uint8).reshape(r // 512, 16, m))


B, N, T, D, NQ = 1, 512, 2048, 1024, 512


def setup_inputs():
    n = np.random.standard_normal
    idx = np.random.permutation(T)[:B * N]
    s = mx_kscale(D)[:, None]
    kp = pack_weight(n((D, T)) / s, "e2m1")
    cp = pack_weight(n((D, T)) / s / 12, "e2m1")
    return {
        "qT": (n((B, D, NQ)) * s * (1.00 / np.sqrt(D))).astype(np.float32),
        "k_words": np.ascontiguousarray(kp[0].reshape(1, 2, 128, T, 2).transpose(0, 2, 3, 1, 4)).reshape(1, 128, T, 4),
        "k_scales": kp[1],
        "c_words": np.ascontiguousarray(cp[0].reshape(1, 2, 128, T, 2).transpose(0, 2, 3, 1, 4)).reshape(1, 128, T, 4),
        "c_scales": cp[1],
        "ls": (np.random.uniform(7.8, 8.4, (B, 1, NQ))).astype(np.float32),
        "offs": striped(idx),
    }


def reference(qT, k_words, k_scales, c_words, c_scales, ls, offs):
    idx = unstriped(offs)
    pick = lambda x, which: x[:, which].reshape(x.shape[0], B, -1).transpose(1, 0, 2)
    k = unpack_weight(k_words.reshape(1, 128, T, 2, 2).transpose(0, 3, 1, 2, 4).reshape(2, 128, 2 * T), k_scales, "e2m1")
    kg = pick(k, idx)
    c = unpack_weight(c_words.reshape(1, 128, T, 2, 2).transpose(0, 3, 1, 2, 4).reshape(2, 128, 2 * T), c_scales, "e2m1")
    cg = pick(c, idx)
    qq = mxq(f64(qT), 1, "e4m3")
    a = (kg.transpose(0, 2, 1) @ qq) + (cg.transpose(0, 2, 1) @ qq)
    y = np.exp(a - f64(ls))
    Y = y[0]
    words, scales = planes(Y)
    return Y, words, scales

@@ -1,0 +1,178 @@
+from contextlib import ExitStack
+
+import concourse.mybir as mybir
+from concourse.masks import make_identity
+
+F32 = mybir.dt.float32
+BF16 = mybir.dt.bfloat16
+I32 = mybir.dt.int32
+U32 = mybir.dt.uint32
+U16 = mybir.dt.uint16
+U8 = mybir.dt.uint8
+FP8X4 = mybir.dt.float8_e4m3fn_x4
+FP4X4 = mybir.dt.float4_e2m1fn_x4
+ACT = mybir.ActivationFunctionType
+ALU = mybir.AluOpType
+
+P = 128
+N, T, D, NQ = 512, 2048, 1024, 512
+CH = NQ // P
+FLOPS = 2 * 2 * N * D * NQ
+ON_SCALAR = ((0, 1), (1, 0), (1, 1))
+
+
+def tile_attend_plw_resid_topk_kernel(tc, qT, k_words, k_scales, c_words, c_scales, ls, offs, out_0, out_1, out_2):
+    nc = tc.nc
+    with ExitStack() as ctx:
+        keep = ctx.enter_context(tc.tile_pool(name="keep", bufs=1))
+        stage = ctx.enter_context(tc.tile_pool(name="stage", bufs=1))
+        work = ctx.enter_context(tc.tile_pool(name="work", bufs=4))
+        ps_s = ctx.enter_context(tc.psum_pool(name="ps_s", bufs=4))
+        ps_t = ctx.enter_context(tc.psum_pool(name="ps_t", bufs=4))
+
+        offsets = keep.tile([P, N // 16], U16, name="offsets")
+        nc.sync.dma_start(offsets[:], offs)
+
+        kw = keep.tile([P, T], I32, name="kw")
+        cw = keep.tile([P, T], I32, name="cw")
+        lsr = keep.tile([P, P], F32, name="lsr")
+        ident = keep.tile([P, P], F32, name="ident")
+        gs = keep.tile([P, 2, N], U8, name="gs", align_bytes=64)
+        planes = []
+        raw = {}
+
+        def load_q(pool, c, o):
+            raw[c, o] = pool.tile([P, 4, P], F32, name="raw%d%d" % (c, o))
+            rows = qT[0, o * 512:(o + 1) * 512, c * P:(c + 1) * P]
+            nc.sync.dma_start(out=raw[c, o][:], in_=rows.rearrange("(p j) q -> p j q", j=4))
+
+        with tc.tile_pool(name="early", bufs=1) as early:
+            ksw = early.tile([P, T // 4], I32, name="ksw")
+            csw = early.tile([P, T // 4], I32, name="csw")
+            for window, scales in ((ksw, k_scales), (csw, c_scales)):
+                nc.sync.dma_start(out=window[96:P, :], in_=scales.rearrange("o f t -> (o f) t").bitcast(I32))
+                nc.vector.memset(window[0:96, :], 0)
+            nc.sync.dma_start(out=kw[:], in_=k_words.rearrange("a p t b -> p (a t b)").bitcast(I32))
+            load_q(keep, 0, 0)
+            nc.sync.dma_start(out=cw[:], in_=c_words.rearrange("a p t b -> p (a t b)").bitcast(I32))
+
+            nc.gpsimd.memset(lsr[:], 0.0)
+            nc.gpsimd.dma_start(out=lsr[0:CH, :], in_=ls.rearrange("a b (c m) -> (a b c) m", m=P))
+            make_identity(nc, ident[:])
+            for o in range(2):
+                planes.append(keep.tile([P, 2, N], U8, name="plane%d" % o, align_bytes=64))
+                nc.vector.memset(planes[o][:].rearrange("p a n -> p (a n)").bitcast(I32), 0)
+
+            nc.vector.tensor_copy(gs[:, 0, :], ksw[:].bitcast(U8).indirect(offsets[:]))
+            nc.vector.tensor_copy(gs[:, 1, :], csw[:].bitcast(U8).indirect(offsets[:]))
+
+        late = ctx.enter_context(tc.tile_pool(name="late", bufs=1))
+        for o in range(2):
+            for u in range(4):
+                nc.scalar.dma_start(
+                    out=planes[o][32 * u:32 * u + 4].rearrange("p a n -> p (a n)").bitcast(I32),
+                    in_=gs[96 + 16 * o + 4 * u:96 + 16 * o + 4 * u + 4].rearrange("p a n -> p (a n)").bitcast(I32),
+                )
+        for c in range(CH):
+            for o in range(2):
+                if (c, o) != (0, 0):
+                    load_q(late, c, o)
+
+        halves = {}
+
+        def gather_words(a, window):
+            g = keep.tile([P, N], U32, name="g%d" % a)
+            nc.vector.tensor_copy(g[:], window[:].bitcast(U32).indirect(offsets[:]))
+            pairs = g[:].bitcast(U16).rearrange("p (s h) -> p h s", h=2)
+            for o in range(2):
+                halves[a, o] = keep.tile([P, N], U16, name="h%d%d" % (a, o), align_bytes=64)
+                nc.vector.tensor_copy(halves[a, o][:], pairs[:, o, :])
+
+        qb, qc, qs = {}, {}, {}
+
+        def interleave_q(c, o):
+            qb[c, o] = stage.tile([P, P, 4], BF16, name="qb%d%d" % (c, o), align_bytes=64, offset=o * P * 4 * 2)
+            dst = qb[c, o][:].rearrange("p (x i) t -> p x t i", i=4)
+            src = raw[c, o][:].rearrange("p t (x i) -> p x t i", i=4)
+            if (c, o) in ON_SCALAR:
+                nc.scalar.activation(dst, src, ACT.Copy)
+            else:
+                nc.vector.tensor_copy(dst, src)
+
+        def quantise_q(c, o):
+            qc[c, o] = keep.tile([P, P], U32, name="qc%d%d" % (c, o), align_bytes=64)
+            qs[c, o] = keep.tile([P, P], U8, name="qs%d%d" % (c, o), align_bytes=64)
+            nc.vector.quantize_mx(out=qc[c, o][:].bitcast(FP8X4), scales=qs[c, o][:],
+                                  in_=qb[c, o][:].rearrange("p q t -> p (q t)"))
+
+        score = {}
+
+        def product(c, a, o):
+            if (a, o) == (0, 0):
+                score[c] = ps_s.tile([P, N], F32, name="score")
+            nc.tensor.matmul_mx(
+                out=score[c][:], lhsT=qc[c, o][:].bitcast(FP8X4), lhsT_scale=qs[c, o][:],
+                rhs=halves[a, o][:].bitcast(FP4X4), rhs_scale=planes[o][:, a, :],
+                start=(a, o) == (0, 0), stop=(a, o) == (1, 1))
+
+        gather_words(0, kw)
+        interleave_q(0, 0)
+        quantise_q(0, 0)
+        product(0, 0, 0)
+
+        lst = ps_t.tile([P, 4, P], F32, name="turned")
+        nc.tensor.transpose(lst[:, 0, :], lsr[:], ident[:])
+        nls = keep.tile([P, CH], F32, name="nls")
+        nc.vector.tensor_scalar(nls[:], lst[:, 0, 0:CH], -1.0, None, ALU.mult)
+
+        gather_words(1, cw)
+
+        yc = keep.tile([P, NQ], U32, name="yc", align_bytes=64)
+        ys = keep.tile([P, NQ], U8, name="ys", align_bytes=64)
+        out_rows = out_0.rearrange("(s r) q -> s r q", r=4)
+        out_words = out_1.rearrange("a p q t -> p (a q t)").bitcast(I32)
+        yT, turned = {}, {}
+
+        def scores(c):
+            for o in range(2):
+                if (c, o) != (0, 0):
+                    interleave_q(c, o)
+                    quantise_q(c, o)
+                    product(c, 0, o)
+                product(c, 1, o)
+            yT[c] = work.tile([P, 4, P], F32, name="yT")
+            nc.scalar.activation(yT[c][:], score[c][:].rearrange("p (s r) -> p r s", r=4), ACT.Exp,
+                                 bias=nls[:, c:c + 1])
+
+        def turn(c):
+            turned[c] = ps_t.tile([P, 4, P], F32, name="turned")
+            for r in range(4):
+                nc.tensor.transpose(turned[c][:, r, :], yT[c][:, r, :], ident[:])
+
+        def finish(c):
+            cols = slice(c * P, (c + 1) * P)
+            y = work.tile([P, 4, P], F32, name="y")
+            yb = work.tile([P, P, 4], BF16, name="yb", align_bytes=64)
+            dst = yb[:].rearrange("p (x i) t -> p x t i", i=4)
+            if c == CH - 1:
+                nc.vector.tensor_copy(dst, turned[c][:].rearrange("p t (x i) -> p x t i", i=4))
+                nc.scalar.copy(y[:], turned[c][:])
+            else:
+                nc.scalar.copy(y[:], turned[c][:])
+                nc.vector.tensor_copy(dst, y[:].rearrange("p t (x i) -> p x t i", i=4))
+            nc.sync.dma_start(out=out_rows[:, :, cols], in_=y[:])
+            nc.vector.quantize_mx(out=yc[:, cols].bitcast(FP8X4), scales=ys[:, cols],
+                                  in_=yb[:].rearrange("p q t -> p (q t)"))
+            nc.sync.dma_start(out=out_words[:, cols], in_=yc[:, cols].bitcast(I32))
+
+        scores(0)
+        for c in range(1, CH):
+            scores(c)
+            turn(c - 1)
+            finish(c - 1)
+        turn(CH - 1)
+        finish(CH - 1)
+        for u in range(4):
+            queue = nc.sync if u % 2 else nc.scalar
+            queue.dma_start(out=out_2[0, 4 * u:4 * u + 4, :].bitcast(I32),
+                            in_=ys[32 * u:32 * u + 4, :].bitcast(I32))

@@ -12,20 +12,19 @@ U8 = mybir.dt.uint8
 FP8X4 = mybir.dt.float8_e4m3fn_x4
 FP4X4 = mybir.dt.float4_e2m1fn_x4
 ACT = mybir.ActivationFunctionType
-ALU = mybir.AluOpType
 
 P = 128
 N, T, D, NQ = 512, 2048, 1024, 512
 CH = NQ // P
 FLOPS = 2 * 2 * N * D * NQ
-ON_SCALAR = ((0, 1), (1, 0), (1, 1))
+SLOT = P * 4 * 2
+ON_SCALAR = ((0, 0), (1, 0), (0, 1), (1, 1), (2, 0), (2, 1))
 
 
 def tile_attend_plw_resid_topk_kernel(tc, qT, k_words, k_scales, c_words, c_scales, ls, offs, out_0, out_1, out_2):
     nc = tc.nc
     with ExitStack() as ctx:
         keep = ctx.enter_context(tc.tile_pool(name="keep", bufs=1))
-        stage = ctx.enter_context(tc.tile_pool(name="stage", bufs=1))
         work = ctx.enter_context(tc.tile_pool(name="work", bufs=4))
         ps_s = ctx.enter_context(tc.psum_pool(name="ps_s", bufs=4))
         ps_t = ctx.enter_context(tc.psum_pool(name="ps_t", bufs=4))
@@ -34,17 +33,40 @@ def tile_attend_plw_resid_topk_kernel(tc, qT, k_words, k_scales, c_words, c_scal
         nc.sync.dma_start(offsets[:], offs)
 
         kw = keep.tile([P, T], I32, name="kw")
-        cw = keep.tile([P, T], I32, name="cw")
         lsr = keep.tile([P, P], F32, name="lsr")
         ident = keep.tile([P, P], F32, name="ident")
         gs = keep.tile([P, 2, N], U8, name="gs", align_bytes=64)
         planes = []
         raw = {}
 
-        def load_q(pool, c, o):
-            raw[c, o] = pool.tile([P, 4, P], F32, name="raw%d%d" % (c, o))
-            rows = qT[0, o * 512:(o + 1) * 512, c * P:(c + 1) * P]
-            nc.sync.dma_start(out=raw[c, o][:], in_=rows.rearrange("(p j) q -> p j q", j=4))
+        def late_offset(c, o):
+            return T * 4 + (2 * (c - 2) + o) * 4 * P * 4
+
+        def load_q(pool, c, n, o, **where):
+            piece = pool.tile([P, 4, n * P], F32, name="raw%d%d" % (c, o), **where)
+            rows = qT[0, o * 512:(o + 1) * 512, c * P:(c + n) * P]
+            nc.sync.dma_start(out=piece[:], in_=rows.rearrange("(p j) q -> p j q", j=4))
+            for i in range(n):
+                raw[c + i, o] = piece[:, :, i * P:(i + 1) * P]
+
+        def place(o):
+            for u in range(4):
+                nc.sync.dma_start(
+                    out=planes[o][32 * u:32 * u + 4].rearrange("p a n -> p (a n)").bitcast(I32),
+                    in_=gs[96 + 16 * o + 4 * u:96 + 16 * o + 4 * u + 4].rearrange("p a n -> p (a n)").bitcast(I32),
+                )
+
+        halves = {}
+
+        def gather_words(a, window):
+            with tc.tile_pool(name="gathered%d" % a, bufs=1) as pool:
+                g = pool.tile([P, N], U32, name="g%d" % a)
+                nc.vector.tensor_copy(g[:], window[:].bitcast(U32).indirect(offsets[:]))
+                pairs = g[:].bitcast(U16).rearrange("p (s h) -> p h s", h=2)
+                for o in range(2):
+                    halves[a, o] = keep.tile([P, N], U16, name="h%d%d" % (a, o), align_bytes=64)
+                    nc.vector.tensor_copy(halves[a, o][:], pairs[:, o, :])
+            return ctx.enter_context(tc.tile_pool(name="after%d" % a, bufs=1))
 
         with tc.tile_pool(name="early", bufs=1) as early:
             ksw = early.tile([P, T // 4], I32, name="ksw")
@@ -53,54 +75,45 @@ def tile_attend_plw_resid_topk_kernel(tc, qT, k_words, k_scales, c_words, c_scal
                 nc.sync.dma_start(out=window[96:P, :], in_=scales.rearrange("o f t -> (o f) t").bitcast(I32))
                 nc.vector.memset(window[0:96, :], 0)
             nc.sync.dma_start(out=kw[:], in_=k_words.rearrange("a p t b -> p (a t b)").bitcast(I32))
-            load_q(keep, 0, 0)
-            nc.sync.dma_start(out=cw[:], in_=c_words.rearrange("a p t b -> p (a t b)").bitcast(I32))
+            load_q(keep, 0, 2, 0)
+            load_q(keep, 0, 2, 1)
+            for o in range(2):
+                planes.append(keep.tile([P, 2, N], U8, name="plane%d" % o, align_bytes=64))
+                nc.vector.memset(planes[o][:].rearrange("p a n -> p (a n)").bitcast(I32), 0)
 
             nc.gpsimd.memset(lsr[:], 0.0)
             nc.gpsimd.dma_start(out=lsr[0:CH, :], in_=ls.rearrange("a b (c m) -> (a b c) m", m=P))
             make_identity(nc, ident[:])
-            for o in range(2):
-                planes.append(keep.tile([P, 2, N], U8, name="plane%d" % o, align_bytes=64))
-                nc.vector.memset(planes[o][:].rearrange("p a n -> p (a n)").bitcast(I32), 0)
 
             nc.vector.tensor_copy(gs[:, 0, :], ksw[:].bitcast(U8).indirect(offsets[:]))
             nc.vector.tensor_copy(gs[:, 1, :], csw[:].bitcast(U8).indirect(offsets[:]))
 
         late = ctx.enter_context(tc.tile_pool(name="late", bufs=1))
-        for o in range(2):
-            for u in range(4):
-                nc.scalar.dma_start(
-                    out=planes[o][32 * u:32 * u + 4].rearrange("p a n -> p (a n)").bitcast(I32),
-                    in_=gs[96 + 16 * o + 4 * u:96 + 16 * o + 4 * u + 4].rearrange("p a n -> p (a n)").bitcast(I32),
-                )
-        for c in range(CH):
+        cw = late.tile([P, T], I32, name="cw", offset=0)
+        place(0)
+        nc.sync.dma_start(out=cw[:], in_=c_words.rearrange("a p t b -> p (a t b)").bitcast(I32))
+        place(1)
+        for c in range(2, CH):
             for o in range(2):
-                if (c, o) != (0, 0):
-                    load_q(late, c, o)
-
-        halves = {}
-
-        def gather_words(a, window):
-            g = keep.tile([P, N], U32, name="g%d" % a)
-            nc.vector.tensor_copy(g[:], window[:].bitcast(U32).indirect(offsets[:]))
-            pairs = g[:].bitcast(U16).rearrange("p (s h) -> p h s", h=2)
-            for o in range(2):
-                halves[a, o] = keep.tile([P, N], U16, name="h%d%d" % (a, o), align_bytes=64)
-                nc.vector.tensor_copy(halves[a, o][:], pairs[:, o, :])
+                load_q(late, c, 1, o, offset=late_offset(c, o))
+        after = [gather_words(0, kw)]
 
         qb, qc, qs = {}, {}, {}
 
         def interleave_q(c, o):
-            qb[c, o] = stage.tile([P, P, 4], BF16, name="qb%d%d" % (c, o), align_bytes=64, offset=o * P * 4 * 2)
+            if (c, o) in ON_SCALAR:
+                qb[c, o] = keep.tile([P, P, 4], BF16, name="qb%d%d" % (c, o), align_bytes=64)
+            else:
+                qb[c, o] = after[1].tile([P, P, 4], BF16, name="qb%d%d" % (c, o), align_bytes=64, offset=o * SLOT)
             dst = qb[c, o][:].rearrange("p (x i) t -> p x t i", i=4)
-            src = raw[c, o][:].rearrange("p t (x i) -> p x t i", i=4)
+            src = raw[c, o].rearrange("p t (x i) -> p x t i", i=4)
             if (c, o) in ON_SCALAR:
                 nc.scalar.activation(dst, src, ACT.Copy)
             else:
                 nc.vector.tensor_copy(dst, src)
 
         def quantise_q(c, o):
-            qc[c, o] = keep.tile([P, P], U32, name="qc%d%d" % (c, o), align_bytes=64)
+            qc[c, o] = after[-1].tile([P, P], U32, name="qc%d%d" % (c, o), align_bytes=64, offset=2 * SLOT + (2 * c + o) * P * 4)
             qs[c, o] = keep.tile([P, P], U8, name="qs%d%d" % (c, o), align_bytes=64)
             nc.vector.quantize_mx(out=qc[c, o][:].bitcast(FP8X4), scales=qs[c, o][:],
                                   in_=qb[c, o][:].rearrange("p q t -> p (q t)"))
@@ -115,17 +128,18 @@ def tile_attend_plw_resid_topk_kernel(tc, qT, k_words, k_scales, c_words, c_scal
                 rhs=halves[a, o][:].bitcast(FP4X4), rhs_scale=planes[o][:, a, :],
                 start=(a, o) == (0, 0), stop=(a, o) == (1, 1))
 
-        gather_words(0, kw)
-        interleave_q(0, 0)
-        quantise_q(0, 0)
-        product(0, 0, 0)
+        for o in range(2):
+            for c in range(2):
+                interleave_q(c, o)
+                quantise_q(c, o)
+                product(c, 0, o)
 
         lst = ps_t.tile([P, 4, P], F32, name="turned")
         nc.tensor.transpose(lst[:, 0, :], lsr[:], ident[:])
-        nls = keep.tile([P, CH], F32, name="nls")
-        nc.vector.tensor_scalar(nls[:], lst[:, 0, 0:CH], -1.0, None, ALU.mult)
+        nls = after[0].tile([P, CH], F32, name="nls", offset=0)
+        nc.vector.tensor_scalar(nls[:], lst[:, 0, 0:CH], -1.0, None, mybir.AluOpType.mult)
 
-        gather_words(1, cw)
+        after.append(gather_words(1, cw))
 
         yc = keep.tile([P, NQ], U32, name="yc", align_bytes=64)
         ys = keep.tile([P, NQ], U8, name="ys", align_bytes=64)
@@ -133,44 +147,74 @@ def tile_attend_plw_resid_topk_kernel(tc, qT, k_words, k_scales, c_words, c_scal
         out_words = out_1.rearrange("a p q t -> p (a q t)").bitcast(I32)
         yT, turned = {}, {}
 
-        def scores(c):
-            for o in range(2):
-                if (c, o) != (0, 0):
-                    interleave_q(c, o)
-                    quantise_q(c, o)
-                    product(c, 0, o)
-                product(c, 1, o)
-            yT[c] = work.tile([P, 4, P], F32, name="yT")
-            nc.scalar.activation(yT[c][:], score[c][:].rearrange("p (s r) -> p r s", r=4), ACT.Exp,
-                                 bias=nls[:, c:c + 1])
+        def weights(c):
+            if c == 0:
+                yT[c] = late.tile([P, 4, P], F32, name="yT0", offset=late_offset(2, 1))
+            else:
+                yT[c] = work.tile([P, 4, P], F32, name="yT")
+            dealt = score[c][:].rearrange("p (s r) -> p r s", r=4)
+            for r0, n in parts(c):
+                nc.scalar.activation(yT[c][:, r0:r0 + n, :], dealt[:, r0:r0 + n, :], ACT.Exp, bias=nls[:, c:c + 1])
+
+        def parts(c):
+            return ((0, 2), (2, 2)) if c == CH - 1 else ((0, 4),)
 
         def turn(c):
-            turned[c] = ps_t.tile([P, 4, P], F32, name="turned")
-            for r in range(4):
-                nc.tensor.transpose(turned[c][:, r, :], yT[c][:, r, :], ident[:])
+            for r0, n in parts(c):
+                turned[c, r0] = ps_t.tile([P, 4, P], F32, name="turned")
+                for r in range(n):
+                    nc.tensor.transpose(turned[c, r0][:, r, :], yT[c][:, r0 + r, :], ident[:])
 
-        def finish(c):
+        ys32 = {}
+
+        def leave(c):
             cols = slice(c * P, (c + 1) * P)
             y = work.tile([P, 4, P], F32, name="y")
-            yb = work.tile([P, P, 4], BF16, name="yb", align_bytes=64)
-            dst = yb[:].rearrange("p (x i) t -> p x t i", i=4)
-            if c == CH - 1:
-                nc.vector.tensor_copy(dst, turned[c][:].rearrange("p t (x i) -> p x t i", i=4))
-                nc.scalar.copy(y[:], turned[c][:])
-            else:
-                nc.scalar.copy(y[:], turned[c][:])
-                nc.vector.tensor_copy(dst, y[:].rearrange("p t (x i) -> p x t i", i=4))
+            ys32[c] = y
+            for r0, n in parts(c):
+                if r0 + n < 4:
+                    nc.vector.tensor_copy(y[:, r0:r0 + n, :], turned[c, r0][:, 0:n, :])
+                else:
+                    nc.scalar.copy(y[:, r0:r0 + n, :], turned[c, r0][:, 0:n, :])
             nc.sync.dma_start(out=out_rows[:, :, cols], in_=y[:])
-            nc.vector.quantize_mx(out=yc[:, cols].bitcast(FP8X4), scales=ys[:, cols],
-                                  in_=yb[:].rearrange("p q t -> p (q t)"))
-            nc.sync.dma_start(out=out_words[:, cols], in_=yc[:, cols].bitcast(I32))
 
-        scores(0)
-        for c in range(1, CH):
-            scores(c)
+        def finish(c):
+            y = ys32[c]
+            yb = after[1].tile([P, P, 4], BF16, name="yb%d" % c, align_bytes=64, offset=((c + 1) % 2) * SLOT)
+            width = P // len(parts(c))
+            for q0 in range(0, P, width):
+                nc.vector.tensor_copy(yb[:, q0:q0 + width, :].rearrange("p (x i) t -> p x t i", i=4),
+                                      y[:, :, q0:q0 + width].rearrange("p t (x i) -> p x t i", i=4))
+            for q0 in range(0, P, width):
+                part = slice(c * P + q0, c * P + q0 + width)
+                nc.vector.quantize_mx(out=yc[:, part].bitcast(FP8X4), scales=ys[:, part],
+                                      in_=yb[:, q0:q0 + width, :].rearrange("p q t -> p (q t)"))
+            if c % 2:
+                pair = slice((c - 1) * P, (c + 1) * P)
+                nc.sync.dma_start(out=out_words[:, pair], in_=yc[:, pair].bitcast(I32))
+
+        for o in range(2):
+            interleave_q(2, o)
+        for c in range(2):
+            product(c, 1, 0)
+            product(c, 1, 1)
+            weights(c)
+        turn(0)
+        leave(0)
+        for c in range(2, CH):
+            for o in range(2):
+                if c > 2:
+                    interleave_q(c, o)
+                quantise_q(c, o)
+                product(c, 0, o)
+                product(c, 1, o)
+            weights(c)
             turn(c - 1)
-            finish(c - 1)
+            leave(c - 1)
         turn(CH - 1)
+        for c in range(CH - 1):
+            finish(c)
+        leave(CH - 1)
         finish(CH - 1)
         for u in range(4):
             queue = nc.sync if u % 2 else nc.scalar

@@ -17,205 +17,196 @@ P = 128
 N, T, D, NQ = 512, 2048, 1024, 512
 CH = NQ // P
 FLOPS = 2 * 2 * N * D * NQ
-SLOT = P * 4 * 2
-ON_SCALAR = ((0, 0), (1, 0), (0, 1), (1, 1), (2, 0), (2, 1))
+KIB = 1024
 
 
 def tile_attend_plw_resid_topk_kernel(tc, qT, k_words, k_scales, c_words, c_scales, ls, offs, out_0, out_1, out_2):
     nc = tc.nc
     with ExitStack() as ctx:
         keep = ctx.enter_context(tc.tile_pool(name="keep", bufs=1))
-        work = ctx.enter_context(tc.tile_pool(name="work", bufs=4))
-        ps_s = ctx.enter_context(tc.psum_pool(name="ps_s", bufs=4))
-        ps_t = ctx.enter_context(tc.psum_pool(name="ps_t", bufs=4))
+        arena = ctx.enter_context(tc.tile_pool(name="arena", bufs=1))
+        psum = ctx.enter_context(tc.psum_pool(name="psum", bufs=1))
 
         offsets = keep.tile([P, N // 16], U16, name="offsets")
         nc.sync.dma_start(offsets[:], offs)
 
-        kw = keep.tile([P, T], I32, name="kw")
-        lsr = keep.tile([P, P], F32, name="lsr")
-        ident = keep.tile([P, P], F32, name="ident")
-        gs = keep.tile([P, 2, N], U8, name="gs", align_bytes=64)
-        planes = []
-        raw = {}
+        KW_AT = 0
+        WIN_AT = 8 * KIB
+        G_AT = 12 * KIB
+        Z_AT = 14 * KIB
 
-        def late_offset(c, o):
-            return T * 4 + (2 * (c - 2) + o) * 4 * P * 4
+        windows = []
+        for a, scales in enumerate((k_scales, c_scales)):
+            window = arena.tile([P, T // 4], I32, name="window%d" % a, offset=WIN_AT + a * T, align_bytes=64)
+            nc.sync.dma_start(out=window[96:P, :], in_=scales.rearrange("o f t -> f o t").bitcast(I32))
+            nc.vector.memset(window[0:96, :], 0)
+            windows.append(window)
+        ls_cols = keep.tile([P, 4], F32, name="ls_cols")
+        nc.sync.dma_start(out=ls_cols[:], in_=ls.rearrange("a b (p j) -> p (a b j)", j=4))
+        ident = keep.tile([P, P], F32, name="ident")
+        make_identity(nc, ident[:])
+
+        raw = {}
 
         def load_q(pool, c, n, o, **where):
             piece = pool.tile([P, 4, n * P], F32, name="raw%d%d" % (c, o), **where)
             rows = qT[0, o * 512:(o + 1) * 512, c * P:(c + n) * P]
             nc.sync.dma_start(out=piece[:], in_=rows.rearrange("(p j) q -> p j q", j=4))
-            for i in range(n):
-                raw[c + i, o] = piece[:, :, i * P:(i + 1) * P]
+            raw[c, o] = piece
 
-        def place(o):
-            for u in range(4):
-                nc.sync.dma_start(
-                    out=planes[o][32 * u:32 * u + 4].rearrange("p a n -> p (a n)").bitcast(I32),
-                    in_=gs[96 + 16 * o + 4 * u:96 + 16 * o + 4 * u + 4].rearrange("p a n -> p (a n)").bitcast(I32),
-                )
+        kw = arena.tile([P, T], I32, name="kw", offset=KW_AT, align_bytes=64)
+        cw = keep.tile([P, T], I32, name="cw")
+        nc.sync.dma_start(out=kw[:], in_=k_words.rearrange("a p t b -> p (a t b)").bitcast(I32))
+        load_q(keep, 0, 2, 0)
+        nc.sync.dma_start(out=cw[:], in_=c_words.rearrange("a p t b -> p (a t b)").bitcast(I32))
+
+        planes = keep.tile([P, 2, 2, N], U8, name="planes", align_bytes=64)
+        nc.vector.memset(planes[:].rearrange("p o a n -> p (o a n)").bitcast(I32), 0)
+
+        gs = keep.tile([P, 2, N], U8, name="gs", align_bytes=64)
+        for a in range(2):
+            nc.vector.tensor_copy(gs[:, a, :], windows[a][:].bitcast(U8).indirect(offsets[:]))
+        dealt = keep.tile([P, 2, 4, P], U8, name="dealt", align_bytes=64)
+        nc.vector.tensor_copy(dealt[:], gs[:].rearrange("p a (s r) -> p a r s", r=4))
+        for u in range(4):
+            nc.sync.dma_start(
+                out=planes[32 * u:32 * u + 4].rearrange("p o a n -> p o (a n)").bitcast(I32),
+                in_=dealt[96 + 8 * u:96 + 8 * u + 8].rearrange("p a r s -> p (a r s)").bitcast(I32),
+            )
+        load_q(arena, 0, 2, 1, offset=WIN_AT, align_bytes=64)
+
+        ls_bank = psum.tile([P, 4, P], F32, name="ls_bank")
+        for j in range(4):
+            nc.tensor.transpose(ls_bank[:, j, :], ls_cols[:, j:j + 1].to_broadcast([P, P]), ident[:])
+        ls_rows = keep.tile([P, NQ], F32, name="ls_rows")
+        nc.scalar.copy(ls_rows[:].rearrange("p (n j) -> p n j", j=4), ls_bank[:].rearrange("p j n -> p n j"))
 
         halves = {}
 
-        def gather_words(a, window):
-            with tc.tile_pool(name="gathered%d" % a, bufs=1) as pool:
-                g = pool.tile([P, N], U32, name="g%d" % a)
-                nc.vector.tensor_copy(g[:], window[:].bitcast(U32).indirect(offsets[:]))
-                pairs = g[:].bitcast(U16).rearrange("p (s h) -> p h s", h=2)
-                for o in range(2):
-                    halves[a, o] = keep.tile([P, N], U16, name="h%d%d" % (a, o), align_bytes=64)
-                    nc.vector.tensor_copy(halves[a, o][:], pairs[:, o, :])
-            return ctx.enter_context(tc.tile_pool(name="after%d" % a, bufs=1))
+        def gather_words(a, window, pool, passes, **where):
+            g = pool.tile([P, N], U32, name="g%d" % a, **where)
+            nc.vector.tensor_copy(g[:], window[:].bitcast(U32).indirect(offsets[:]))
+            pairs = g[:].bitcast(U16).rearrange("p (s r h) -> p h s r", h=2, r=4)
+            halves[a] = keep.tile([P, 2, 4, P], U16, name="h%d" % a, align_bytes=64)
+            for lo, hi in passes:
+                nc.vector.tensor_copy(halves[a][:, lo:hi].rearrange("p h r s -> p h s r"), pairs[:, lo:hi])
 
-        with tc.tile_pool(name="early", bufs=1) as early:
-            ksw = early.tile([P, T // 4], I32, name="ksw")
-            csw = early.tile([P, T // 4], I32, name="csw")
-            for window, scales in ((ksw, k_scales), (csw, c_scales)):
-                nc.sync.dma_start(out=window[96:P, :], in_=scales.rearrange("o f t -> (o f) t").bitcast(I32))
-                nc.vector.memset(window[0:96, :], 0)
-            nc.sync.dma_start(out=kw[:], in_=k_words.rearrange("a p t b -> p (a t b)").bitcast(I32))
-            load_q(keep, 0, 2, 0)
-            load_q(keep, 0, 2, 1)
-            for o in range(2):
-                planes.append(keep.tile([P, 2, N], U8, name="plane%d" % o, align_bytes=64))
-                nc.vector.memset(planes[o][:].rearrange("p a n -> p (a n)").bitcast(I32), 0)
-
-            nc.gpsimd.memset(lsr[:], 0.0)
-            nc.gpsimd.dma_start(out=lsr[0:CH, :], in_=ls.rearrange("a b (c m) -> (a b c) m", m=P))
-            make_identity(nc, ident[:])
-
-            nc.vector.tensor_copy(gs[:, 0, :], ksw[:].bitcast(U8).indirect(offsets[:]))
-            nc.vector.tensor_copy(gs[:, 1, :], csw[:].bitcast(U8).indirect(offsets[:]))
-
-        late = ctx.enter_context(tc.tile_pool(name="late", bufs=1))
-        cw = late.tile([P, T], I32, name="cw", offset=0)
-        place(0)
-        nc.sync.dma_start(out=cw[:], in_=c_words.rearrange("a p t b -> p (a t b)").bitcast(I32))
-        place(1)
-        for c in range(2, CH):
-            for o in range(2):
-                load_q(late, c, 1, o, offset=late_offset(c, o))
-        after = [gather_words(0, kw)]
-
-        qb, qc, qs = {}, {}, {}
-
-        def interleave_q(c, o):
-            if (c, o) in ON_SCALAR:
-                qb[c, o] = keep.tile([P, P, 4], BF16, name="qb%d%d" % (c, o), align_bytes=64)
-            else:
-                qb[c, o] = after[1].tile([P, P, 4], BF16, name="qb%d%d" % (c, o), align_bytes=64, offset=o * SLOT)
-            dst = qb[c, o][:].rearrange("p (x i) t -> p x t i", i=4)
-            src = raw[c, o].rearrange("p t (x i) -> p x t i", i=4)
-            if (c, o) in ON_SCALAR:
+        def interleave(engine, dst, src):
+            dst = dst.rearrange("p (x i) t -> p x t i", i=4)
+            src = src.rearrange("p t (x i) -> p x t i", i=4)
+            if engine == "scalar":
                 nc.scalar.activation(dst, src, ACT.Copy)
             else:
                 nc.vector.tensor_copy(dst, src)
 
-        def quantise_q(c, o):
-            qc[c, o] = after[-1].tile([P, P], U32, name="qc%d%d" % (c, o), align_bytes=64, offset=2 * SLOT + (2 * c + o) * P * 4)
-            qs[c, o] = keep.tile([P, P], U8, name="qs%d%d" % (c, o), align_bytes=64)
-            nc.vector.quantize_mx(out=qc[c, o][:].bitcast(FP8X4), scales=qs[c, o][:],
+        qb, qc = {}, {}
+        qs = keep.tile([P, 2, NQ], U8, name="qs", align_bytes=64)
+
+        def round_q(engine, c, n, o, src, pool, **where):
+            qb[c, o] = pool.tile([P, n * P, 4], BF16, name="qb%d%d" % (c, o), align_bytes=64, **where)
+            interleave(engine, qb[c, o][:], src)
+
+        def quantise_q(c, n, o, codes):
+            nc.vector.quantize_mx(out=codes.bitcast(FP8X4), scales=qs[:, o, c * P:(c + n) * P],
                                   in_=qb[c, o][:].rearrange("p q t -> p (q t)"))
 
-        score = {}
-
-        def product(c, a, o):
-            if (a, o) == (0, 0):
-                score[c] = ps_s.tile([P, N], F32, name="score")
+        def product(out, c, n, a, o, r, start, stop):
             nc.tensor.matmul_mx(
-                out=score[c][:], lhsT=qc[c, o][:].bitcast(FP8X4), lhsT_scale=qs[c, o][:],
-                rhs=halves[a, o][:].bitcast(FP4X4), rhs_scale=planes[o][:, a, :],
-                start=(a, o) == (0, 0), stop=(a, o) == (1, 1))
-
-        for o in range(2):
-            for c in range(2):
-                interleave_q(c, o)
-                quantise_q(c, o)
-                product(c, 0, o)
-
-        lst = ps_t.tile([P, 4, P], F32, name="turned")
-        nc.tensor.transpose(lst[:, 0, :], lsr[:], ident[:])
-        nls = after[0].tile([P, CH], F32, name="nls", offset=0)
-        nc.vector.tensor_scalar(nls[:], lst[:, 0, 0:CH], -1.0, None, mybir.AluOpType.mult)
-
-        after.append(gather_words(1, cw))
+                out=out, lhsT=halves[a][:, o, r, :].bitcast(FP4X4), lhsT_scale=planes[:, o, a, r * P:(r + 1) * P],
+                rhs=qc[c, o][:].bitcast(FP8X4), rhs_scale=qs[:, o, c * P:(c + n) * P], start=start, stop=stop)
 
         yc = keep.tile([P, NQ], U32, name="yc", align_bytes=64)
         ys = keep.tile([P, NQ], U8, name="ys", align_bytes=64)
         out_rows = out_0.rearrange("(s r) q -> s r q", r=4)
         out_words = out_1.rearrange("a p q t -> p (a q t)").bitcast(I32)
-        yT, turned = {}, {}
 
-        def weights(c):
-            if c == 0:
-                yT[c] = late.tile([P, 4, P], F32, name="yT0", offset=late_offset(2, 1))
-            else:
-                yT[c] = work.tile([P, 4, P], F32, name="yT")
-            dealt = score[c][:].rearrange("p (s r) -> p r s", r=4)
-            for r0, n in parts(c):
-                nc.scalar.activation(yT[c][:, r0:r0 + n, :], dealt[:, r0:r0 + n, :], ACT.Exp, bias=nls[:, c:c + 1])
+        def subtract(bank, c, n, pool, name, **where):
+            rows = bank.shape[1]
+            z = pool.tile([P, rows, n * P], F32, name=name, **where)
+            spread = ls_rows[:, c * P:(c + n) * P].unsqueeze(1).to_broadcast([P, rows, n * P])
+            nc.vector.tensor_tensor(z[:], bank[:], spread, mybir.AluOpType.subtract)
+            return z
 
-        def parts(c):
-            return ((0, 2), (2, 2)) if c == CH - 1 else ((0, 4),)
+        def weights(y, z, c, n, r0):
+            rows = slice(r0, r0 + z.shape[1])
+            nc.scalar.activation(y[:, rows, :], z[:], ACT.Exp)
+            nc.sync.dma_start(out=out_rows[:, rows, c * P:(c + n) * P], in_=y[:, rows, :])
 
-        def turn(c):
-            for r0, n in parts(c):
-                turned[c, r0] = ps_t.tile([P, 4, P], F32, name="turned")
-                for r in range(n):
-                    nc.tensor.transpose(turned[c, r0][:, r, :], yT[c][:, r0 + r, :], ident[:])
+        yb = {}
 
-        ys32 = {}
+        def round_y(engine, y, c, n):
+            yb[c] = keep.tile([P, n * P, 4], BF16, name="yb%d" % c, align_bytes=64)
+            interleave(engine, yb[c][:], y[:])
 
-        def leave(c):
-            cols = slice(c * P, (c + 1) * P)
-            y = work.tile([P, 4, P], F32, name="y")
-            ys32[c] = y
-            for r0, n in parts(c):
-                if r0 + n < 4:
-                    nc.vector.tensor_copy(y[:, r0:r0 + n, :], turned[c, r0][:, 0:n, :])
-                else:
-                    nc.scalar.copy(y[:, r0:r0 + n, :], turned[c, r0][:, 0:n, :])
-            nc.sync.dma_start(out=out_rows[:, :, cols], in_=y[:])
+        def quantise_y(c, n):
+            cols = slice(c * P, (c + n) * P)
+            nc.vector.quantize_mx(out=yc[:, cols].bitcast(FP8X4), scales=ys[:, cols],
+                                  in_=yb[c][:].rearrange("p q t -> p (q t)"))
 
-        def finish(c):
-            y = ys32[c]
-            yb = after[1].tile([P, P, 4], BF16, name="yb%d" % c, align_bytes=64, offset=((c + 1) % 2) * SLOT)
-            width = P // len(parts(c))
-            for q0 in range(0, P, width):
-                nc.vector.tensor_copy(yb[:, q0:q0 + width, :].rearrange("p (x i) t -> p x t i", i=4),
-                                      y[:, :, q0:q0 + width].rearrange("p t (x i) -> p x t i", i=4))
-            for q0 in range(0, P, width):
-                part = slice(c * P + q0, c * P + q0 + width)
-                nc.vector.quantize_mx(out=yc[:, part].bitcast(FP8X4), scales=ys[:, part],
-                                      in_=yb[:, q0:q0 + width, :].rearrange("p q t -> p (q t)"))
-            if c % 2:
-                pair = slice((c - 1) * P, (c + 1) * P)
-                nc.sync.dma_start(out=out_words[:, pair], in_=yc[:, pair].bitcast(I32))
+        def store_words(c):
+            pair = slice(c * P, (c + 2) * P)
+            nc.sync.dma_start(out=out_words[:, pair], in_=yc[:, pair].bitcast(I32))
 
-        for o in range(2):
-            interleave_q(2, o)
-        for c in range(2):
-            product(c, 1, 0)
-            product(c, 1, 1)
-            weights(c)
-        turn(0)
-        leave(0)
-        for c in range(2, CH):
+        gather_words(0, kw, keep, ((0, 2),))
+        for c in (2, 3):
             for o in range(2):
-                if c > 2:
-                    interleave_q(c, o)
-                quantise_q(c, o)
-                product(c, 0, o)
-                product(c, 1, o)
-            weights(c)
-            turn(c - 1)
-            leave(c - 1)
-        turn(CH - 1)
-        for c in range(CH - 1):
-            finish(c)
-        leave(CH - 1)
-        finish(CH - 1)
+                load_q(arena, c, 1, o, offset=KW_AT + (2 * (c - 2) + o) * 2 * KIB, align_bytes=64)
+        round_q("scalar", 0, 2, 0, raw[0, 0][:], arena, offset=G_AT)
+        qc[0, 0] = keep.tile([P, 2 * P], U32, name="qc00", align_bytes=64)
+        quantise_q(0, 2, 0, qc[0, 0][:])
+        banks = [psum.tile([P, 2, 2 * P], F32, name="bank%d" % b) for b in range(2)]
+        for r in range(4):
+            product(banks[r // 2][:, r % 2, :], 0, 2, 0, 0, r, r % 2 == 0, False)
+        gather_words(1, cw, arena, ((0, 1), (1, 2)), offset=G_AT, align_bytes=64)
+        for r in range(4):
+            product(banks[r // 2][:, r % 2, :], 0, 2, 1, 0, r, False, False)
+        round_q("scalar", 0, 1, 1, raw[0, 1][:, :, 0:P], keep)
+        round_q("vector", 1, 1, 1, raw[0, 1][:, :, P:2 * P], arena, offset=G_AT)
+        qc[0, 1] = arena.tile([P, 2 * P], U32, name="qc01", align_bytes=64, offset=G_AT + KIB)
+        quantise_q(0, 1, 1, qc[0, 1][:, 0:P])
+        quantise_q(1, 1, 1, qc[0, 1][:, P:2 * P])
+        for r in range(4):
+            for a in range(2):
+                product(banks[r // 2][:, r % 2, :], 0, 2, a, 1, r, False, r % 2 == 1 and a == 1)
+
+        def late_q(c, o, pool, **where):
+            round_q("scalar", c, 1, o, raw[c, o][:], pool, **where)
+            qc[c, o] = keep.tile([P, P], U32, name="qc%d%d" % (c, o), align_bytes=64)
+            quantise_q(c, 1, o, qc[c, o][:])
+
+        def late_products(c):
+            bank = psum.tile([P, 4, P], F32, name="bank%d" % c)
+            for r in range(4):
+                for o in range(2):
+                    for a in range(2):
+                        product(bank[:, r, :], c, 1, a, o, r, (o, a) == (0, 0), (o, a) == (1, 1))
+            return bank
+
+        late_q(2, 0, keep)
+        late_q(2, 1, arena, offset=Z_AT)
+        z0 = subtract(banks[0], 0, 2, arena, "z0", offset=Z_AT, align_bytes=64)
+        bank_c = late_products(2)
+        late_q(3, 0, keep)
+        z1 = subtract(banks[1], 0, 2, keep, "z1")
+        late_q(3, 1, keep)
+        bank_d = late_products(3)
+        y01 = arena.tile([P, 4, 2 * P], F32, name="y01", offset=KW_AT + 4 * KIB, align_bytes=64)
+        weights(y01, z0, 0, 2, 0)
+        weights(y01, z1, 0, 2, 2)
+        z2 = subtract(bank_c, 2, 1, keep, "z2")
+        y2 = keep.tile([P, 4, P], F32, name="y2")
+        weights(y2, z2, 2, 1, 0)
+        round_y("vector", y01, 0, 2)
+        z3 = subtract(bank_d, 3, 1, keep, "z3")
+        round_y("scalar", y2, 2, 1)
+        y3 = keep.tile([P, 4, P], F32, name="y3")
+        weights(y3, z3, 3, 1, 0)
+        quantise_y(0, 2)
+        store_words(0)
+        quantise_y(2, 1)
+        round_y("vector", y3, 3, 1)
+        quantise_y(3, 1)
+        store_words(2)
         for u in range(4):
             queue = nc.sync if u % 2 else nc.scalar
             queue.dma_start(out=out_2[0, 4 * u:4 * u + 4, :].bitcast(I32),

@@ -31,9 +31,8 @@ def tile_attend_plw_resid_topk_kernel(tc, qT, k_words, k_scales, c_words, c_scal
         nc.sync.dma_start(offsets[:], offs)
 
         KW_AT = 0
+        Q0_AT = 12 * KIB
         WIN_AT = 8 * KIB
-        G_AT = 12 * KIB
-        Z_AT = 14 * KIB
 
         windows = []
         for a, scales in enumerate((k_scales, c_scales)):
@@ -57,7 +56,7 @@ def tile_attend_plw_resid_topk_kernel(tc, qT, k_words, k_scales, c_words, c_scal
         kw = arena.tile([P, T], I32, name="kw", offset=KW_AT, align_bytes=64)
         cw = keep.tile([P, T], I32, name="cw")
         nc.sync.dma_start(out=kw[:], in_=k_words.rearrange("a p t b -> p (a t b)").bitcast(I32))
-        load_q(keep, 0, 2, 0)
+        load_q(arena, 0, 2, 0, offset=Q0_AT, align_bytes=64)
         nc.sync.dma_start(out=cw[:], in_=c_words.rearrange("a p t b -> p (a t b)").bitcast(I32))
 
         planes = keep.tile([P, 2, 2, N], U8, name="planes", align_bytes=64)
@@ -67,7 +66,8 @@ def tile_attend_plw_resid_topk_kernel(tc, qT, k_words, k_scales, c_words, c_scal
         for a in range(2):
             nc.vector.tensor_copy(gs[:, a, :], windows[a][:].bitcast(U8).indirect(offsets[:]))
         dealt = keep.tile([P, 2, 4, P], U8, name="dealt", align_bytes=64)
-        nc.vector.tensor_copy(dealt[:], gs[:].rearrange("p a (s r) -> p a r s", r=4))
+        for a in range(2):
+            nc.vector.tensor_copy(dealt[:, a], gs[:, a, :].rearrange("p (s r) -> p r s", r=4))
         for u in range(4):
             nc.sync.dma_start(
                 out=planes[32 * u:32 * u + 4].rearrange("p o a n -> p o (a n)").bitcast(I32),
@@ -83,13 +83,17 @@ def tile_attend_plw_resid_topk_kernel(tc, qT, k_words, k_scales, c_words, c_scal
 
         halves = {}
 
-        def gather_words(a, window, pool, passes, **where):
-            g = pool.tile([P, N], U32, name="g%d" % a, **where)
-            nc.vector.tensor_copy(g[:], window[:].bitcast(U32).indirect(offsets[:]))
-            pairs = g[:].bitcast(U16).rearrange("p (s r h) -> p h s r", h=2, r=4)
+        def gather_words(a, window, pool, at=None):
             halves[a] = keep.tile([P, 2, 4, P], U16, name="h%d" % a, align_bytes=64)
-            for lo, hi in passes:
-                nc.vector.tensor_copy(halves[a][:, lo:hi].rearrange("p h r s -> p h s r"), pairs[:, lo:hi])
+            gathered = []
+            for part in range(2):
+                where = {} if at is None else {"offset": at + part * KIB, "align_bytes": 64}
+                g = pool.tile([P, N // 2], U32, name="g%d%d" % (a, part), **where)
+                nc.vector.tensor_copy(g[:], window[:].bitcast(U32).indirect(offsets[:, 16 * part:16 * part + 16]))
+                gathered.append(g)
+            for part in range(2):
+                pairs = gathered[part][:].bitcast(U16).rearrange("p (s r h) -> p h s r", h=2, r=4)
+                nc.vector.tensor_copy(halves[a][:, :, :, 64 * part:64 * part + 64].rearrange("p h r s -> p h s r"), pairs)
 
         def interleave(engine, dst, src):
             dst = dst.rearrange("p (x i) t -> p x t i", i=4)
@@ -134,9 +138,10 @@ def tile_attend_plw_resid_topk_kernel(tc, qT, k_words, k_scales, c_words, c_scal
 
         yb = {}
 
-        def round_y(engine, y, c, n):
-            yb[c] = keep.tile([P, n * P, 4], BF16, name="yb%d" % c, align_bytes=64)
-            interleave(engine, yb[c][:], y[:])
+        def round_y(engines, y, c):
+            yb[c] = keep.tile([P, len(engines) * P, 4], BF16, name="yb%d" % c, align_bytes=64)
+            for i, engine in enumerate(engines):
+                interleave(engine, yb[c][:, i * P:(i + 1) * P, :], y[:, :, i * P:(i + 1) * P])
 
         def quantise_y(c, n):
             cols = slice(c * P, (c + n) * P)
@@ -147,22 +152,22 @@ def tile_attend_plw_resid_topk_kernel(tc, qT, k_words, k_scales, c_words, c_scal
             pair = slice(c * P, (c + 2) * P)
             nc.sync.dma_start(out=out_words[:, pair], in_=yc[:, pair].bitcast(I32))
 
-        gather_words(0, kw, keep, ((0, 2),))
+        gather_words(0, kw, keep)
         for c in (2, 3):
             for o in range(2):
                 load_q(arena, c, 1, o, offset=KW_AT + (2 * (c - 2) + o) * 2 * KIB, align_bytes=64)
-        round_q("scalar", 0, 2, 0, raw[0, 0][:], arena, offset=G_AT)
+        round_q("scalar", 0, 2, 0, raw[0, 0][:], keep)
         qc[0, 0] = keep.tile([P, 2 * P], U32, name="qc00", align_bytes=64)
         quantise_q(0, 2, 0, qc[0, 0][:])
         banks = [psum.tile([P, 2, 2 * P], F32, name="bank%d" % b) for b in range(2)]
         for r in range(4):
             product(banks[r // 2][:, r % 2, :], 0, 2, 0, 0, r, r % 2 == 0, False)
-        gather_words(1, cw, arena, ((0, 1), (1, 2)), offset=G_AT, align_bytes=64)
+        gather_words(1, cw, arena, Q0_AT)
         for r in range(4):
             product(banks[r // 2][:, r % 2, :], 0, 2, 1, 0, r, False, False)
         round_q("scalar", 0, 1, 1, raw[0, 1][:, :, 0:P], keep)
-        round_q("vector", 1, 1, 1, raw[0, 1][:, :, P:2 * P], arena, offset=G_AT)
-        qc[0, 1] = arena.tile([P, 2 * P], U32, name="qc01", align_bytes=64, offset=G_AT + KIB)
+        round_q("vector", 1, 1, 1, raw[0, 1][:, :, P:2 * P], keep)
+        qc[0, 1] = keep.tile([P, 2 * P], U32, name="qc01", align_bytes=64)
         quantise_q(0, 1, 1, qc[0, 1][:, 0:P])
         quantise_q(1, 1, 1, qc[0, 1][:, P:2 * P])
         for r in range(4):
@@ -174,37 +179,39 @@ def tile_attend_plw_resid_topk_kernel(tc, qT, k_words, k_scales, c_words, c_scal
             qc[c, o] = keep.tile([P, P], U32, name="qc%d%d" % (c, o), align_bytes=64)
             quantise_q(c, 1, o, qc[c, o][:])
 
-        def late_products(c):
-            bank = psum.tile([P, 4, P], F32, name="bank%d" % c)
-            for r in range(4):
-                for o in range(2):
+        def late_products(c, rows):
+            late = [psum.tile([P, rows, P], F32, name="bank%d_%d" % (c, b)) for b in range(4 // rows)]
+            for o in range(2):
+                for r in range(4):
                     for a in range(2):
-                        product(bank[:, r, :], c, 1, a, o, r, (o, a) == (0, 0), (o, a) == (1, 1))
-            return bank
+                        product(late[r // rows][:, r % rows, :], c, 1, a, o, r,
+                                (o, r % rows, a) == (0, 0, 0), (o, r % rows, a) == (1, rows - 1, 1))
+            return late
 
         late_q(2, 0, keep)
-        late_q(2, 1, arena, offset=Z_AT)
-        z0 = subtract(banks[0], 0, 2, arena, "z0", offset=Z_AT, align_bytes=64)
-        bank_c = late_products(2)
+        late_q(2, 1, keep)
+        z0 = subtract(banks[0], 0, 2, arena, "z0", offset=KW_AT + 2 * KIB, align_bytes=64)
+        bank_c = late_products(2, 4)
         late_q(3, 0, keep)
         z1 = subtract(banks[1], 0, 2, keep, "z1")
         late_q(3, 1, keep)
-        bank_d = late_products(3)
-        y01 = arena.tile([P, 4, 2 * P], F32, name="y01", offset=KW_AT + 4 * KIB, align_bytes=64)
+        bank_d = late_products(3, 2)
+        y01 = arena.tile([P, 4, 2 * P], F32, name="y01", offset=KW_AT + 7 * KIB, align_bytes=64)
         weights(y01, z0, 0, 2, 0)
         weights(y01, z1, 0, 2, 2)
-        z2 = subtract(bank_c, 2, 1, keep, "z2")
+        z2 = subtract(bank_c[0], 2, 1, arena, "z2", offset=KW_AT + 5 * KIB, align_bytes=64)
+        round_y(("scalar", "vector"), y01, 0)
         y2 = keep.tile([P, 4, P], F32, name="y2")
         weights(y2, z2, 2, 1, 0)
-        round_y("vector", y01, 0, 2)
-        z3 = subtract(bank_d, 3, 1, keep, "z3")
-        round_y("scalar", y2, 2, 1)
+        z3 = [subtract(bank_d[b], 3, 1, keep, "z3_%d" % b) for b in range(2)]
         y3 = keep.tile([P, 4, P], F32, name="y3")
-        weights(y3, z3, 3, 1, 0)
+        for b in range(2):
+            weights(y3, z3[b], 3, 1, 2 * b)
         quantise_y(0, 2)
         store_words(0)
+        round_y(("vector",), y2, 2)
+        round_y(("vector",), y3, 3)
         quantise_y(2, 1)
-        round_y("vector", y3, 3, 1)
         quantise_y(3, 1)
         store_words(2)
         for u in range(4):

@@ -32,16 +32,19 @@ def tile_attend_plw_resid_topk_kernel(tc, qT, k_words, k_scales, c_words, c_scal
 
         KW_AT = 0
         Q0_AT = 12 * KIB
+        LS_AT = 16 * KIB
+        Q1_AT = 18 * KIB
+        QC_AT = 20 * KIB
         WIN_AT = 8 * KIB
 
         windows = []
         for a, scales in enumerate((k_scales, c_scales)):
             window = arena.tile([P, T // 4], I32, name="window%d" % a, offset=WIN_AT + a * T, align_bytes=64)
-            nc.sync.dma_start(out=window[96:P, :], in_=scales.rearrange("o f t -> f o t").bitcast(I32))
+            (nc.scalar if a else nc.sync).dma_start(out=window[96:P, :], in_=scales.rearrange("o f t -> f o t").bitcast(I32))
             nc.vector.memset(window[0:96, :], 0)
             windows.append(window)
-        ls_cols = keep.tile([P, 4], F32, name="ls_cols")
-        nc.sync.dma_start(out=ls_cols[:], in_=ls.rearrange("a b (p j) -> p (a b j)", j=4))
+        ls_cols = arena.tile([P, 4], F32, name="ls_cols", offset=LS_AT, align_bytes=64)
+        nc.scalar.dma_start(out=ls_cols[:], in_=ls.rearrange("a b (p j) -> p (a b j)", j=4))
         ident = keep.tile([P, P], F32, name="ident")
         make_identity(nc, ident[:])
 
@@ -58,9 +61,10 @@ def tile_attend_plw_resid_topk_kernel(tc, qT, k_words, k_scales, c_words, c_scal
         nc.sync.dma_start(out=kw[:], in_=k_words.rearrange("a p t b -> p (a t b)").bitcast(I32))
         load_q(arena, 0, 2, 0, offset=Q0_AT, align_bytes=64)
         nc.sync.dma_start(out=cw[:], in_=c_words.rearrange("a p t b -> p (a t b)").bitcast(I32))
+        load_q(arena, 0, 1, 1, offset=Q1_AT, align_bytes=64)
 
         planes = keep.tile([P, 2, 2, N], U8, name="planes", align_bytes=64)
-        nc.vector.memset(planes[:].rearrange("p o a n -> p (o a n)").bitcast(I32), 0)
+        nc.gpsimd.memset(planes[:].rearrange("p o a n -> p (o a n)").bitcast(I32), 0)
 
         gs = keep.tile([P, 2, N], U8, name="gs", align_bytes=64)
         for a in range(2):
@@ -73,7 +77,7 @@ def tile_attend_plw_resid_topk_kernel(tc, qT, k_words, k_scales, c_words, c_scal
                 out=planes[32 * u:32 * u + 4].rearrange("p o a n -> p o (a n)").bitcast(I32),
                 in_=dealt[96 + 8 * u:96 + 8 * u + 8].rearrange("p a r s -> p (a r s)").bitcast(I32),
             )
-        load_q(arena, 0, 2, 1, offset=WIN_AT, align_bytes=64)
+        load_q(arena, 1, 1, 1, offset=WIN_AT + KIB, align_bytes=64)
 
         ls_bank = psum.tile([P, 4, P], F32, name="ls_bank")
         for j in range(4):
@@ -83,17 +87,13 @@ def tile_attend_plw_resid_topk_kernel(tc, qT, k_words, k_scales, c_words, c_scal
 
         halves = {}
 
-        def gather_words(a, window, pool, at=None):
-            halves[a] = keep.tile([P, 2, 4, P], U16, name="h%d" % a, align_bytes=64)
-            gathered = []
-            for part in range(2):
-                where = {} if at is None else {"offset": at + part * KIB, "align_bytes": 64}
-                g = pool.tile([P, N // 2], U32, name="g%d%d" % (a, part), **where)
-                nc.vector.tensor_copy(g[:], window[:].bitcast(U32).indirect(offsets[:, 16 * part:16 * part + 16]))
-                gathered.append(g)
-            for part in range(2):
-                pairs = gathered[part][:].bitcast(U16).rearrange("p (s r h) -> p h s r", h=2, r=4)
-                nc.vector.tensor_copy(halves[a][:, :, :, 64 * part:64 * part + 64].rearrange("p h r s -> p h s r"), pairs)
+        def gather_words(a, window, pool, **where):
+            g = pool.tile([P, N], U32, name="g%d" % a, **where)
+            nc.vector.tensor_copy(g[:], window[:].bitcast(U32).indirect(offsets[:]))
+            return g[:].bitcast(U16).rearrange("p (s r h) -> p h s r", h=2, r=4)
+
+        def part_words(a, pairs, lo, hi):
+            nc.vector.tensor_copy(halves[a][:, lo:hi].rearrange("p h r s -> p h s r"), pairs[:, lo:hi])
 
         def interleave(engine, dst, src):
             dst = dst.rearrange("p (x i) t -> p x t i", i=4)
@@ -119,7 +119,6 @@ def tile_attend_plw_resid_topk_kernel(tc, qT, k_words, k_scales, c_words, c_scal
                 out=out, lhsT=halves[a][:, o, r, :].bitcast(FP4X4), lhsT_scale=planes[:, o, a, r * P:(r + 1) * P],
                 rhs=qc[c, o][:].bitcast(FP8X4), rhs_scale=qs[:, o, c * P:(c + n) * P], start=start, stop=stop)
 
-        yc = keep.tile([P, NQ], U32, name="yc", align_bytes=64)
         ys = keep.tile([P, NQ], U8, name="ys", align_bytes=64)
         out_rows = out_0.rearrange("(s r) q -> s r q", r=4)
         out_words = out_1.rearrange("a p q t -> p (a q t)").bitcast(I32)
@@ -152,32 +151,55 @@ def tile_attend_plw_resid_topk_kernel(tc, qT, k_words, k_scales, c_words, c_scal
             pair = slice(c * P, (c + 2) * P)
             nc.sync.dma_start(out=out_words[:, pair], in_=yc[:, pair].bitcast(I32))
 
-        gather_words(0, kw, keep)
+        halves[0] = keep.tile([P, 2, 4, P], U16, name="h0", align_bytes=64)
+        pairs = gather_words(0, kw, keep)
+        load_q(arena, 2, 2, 0, offset=KW_AT, align_bytes=64)
         for c in (2, 3):
-            for o in range(2):
-                load_q(arena, c, 1, o, offset=KW_AT + (2 * (c - 2) + o) * 2 * KIB, align_bytes=64)
-        round_q("scalar", 0, 2, 0, raw[0, 0][:], keep)
+            load_q(arena, c, 1, 1, offset=KW_AT + c * 2 * KIB, align_bytes=64)
+
+        def round_pair(c, o, parts):
+            qb[c, o] = keep.tile([P, 2 * P, 4], BF16, name="qb%d%d" % (c, o), align_bytes=64)
+            for i, (engine, src) in enumerate(parts):
+                width = src.shape[2]
+                interleave(engine, qb[c, o][:, i * width:(i + 1) * width, :], src)
+            qc[c, o] = keep.tile([P, 2 * P], U32, name="qc%d%d" % (c, o), align_bytes=64)
+            quantise_q(c, 2, o, qc[c, o][:])
+
+        qb[0, 0] = arena.tile([P, 2 * P, 4], BF16, name="qb00", offset=LS_AT, align_bytes=64)
         qc[0, 0] = keep.tile([P, 2 * P], U32, name="qc00", align_bytes=64)
-        quantise_q(0, 2, 0, qc[0, 0][:])
+        for c in range(2):
+            cols = slice(c * P, (c + 1) * P)
+            interleave("scalar", qb[0, 0][:, cols, :], raw[0, 0][:, :, cols])
+            nc.vector.quantize_mx(out=qc[0, 0][:, cols].bitcast(FP8X4), scales=qs[:, 0, cols],
+                                  in_=qb[0, 0][:, cols, :].rearrange("p q t -> p (q t)"))
+            part_words(0, pairs, c, c + 1)
+        spare = psum.tile([P, 2 * P], F32, name="spare")
+        for r in range(2):
+            nc.tensor.matmul_mx(
+                out=spare[:], lhsT=halves[0][:, 0, r, :].bitcast(FP4X4), lhsT_scale=qs[:, 0, 0:P],
+                rhs=qc[0, 0][:].bitcast(FP8X4), rhs_scale=qs[:, 0, 0:2 * P], start=True, stop=True)
         banks = [psum.tile([P, 2, 2 * P], F32, name="bank%d" % b) for b in range(2)]
         for r in range(4):
             product(banks[r // 2][:, r % 2, :], 0, 2, 0, 0, r, r % 2 == 0, False)
-        gather_words(1, cw, arena, Q0_AT)
+        pairs = gather_words(1, cw, arena, offset=Q0_AT, align_bytes=64)
+        qc[0, 1] = arena.tile([P, 2 * P], U32, name="qc01", offset=QC_AT, align_bytes=64)
+        round_q("scalar", 0, 1, 1, raw[0, 1][:], keep)
+        round_q("scalar", 1, 1, 1, raw[1, 1][:], keep)
+        quantise_q(0, 1, 1, qc[0, 1][:, 0:P])
+        halves[1] = arena.tile([P, 2, 4, P], U16, name="h1", offset=Q1_AT, align_bytes=64)
+        part_words(1, pairs, 0, 1)
         for r in range(4):
             product(banks[r // 2][:, r % 2, :], 0, 2, 1, 0, r, False, False)
-        round_q("scalar", 0, 1, 1, raw[0, 1][:, :, 0:P], keep)
-        round_q("vector", 1, 1, 1, raw[0, 1][:, :, P:2 * P], keep)
-        qc[0, 1] = keep.tile([P, 2 * P], U32, name="qc01", align_bytes=64)
-        quantise_q(0, 1, 1, qc[0, 1][:, 0:P])
+        part_words(1, pairs, 1, 2)
         quantise_q(1, 1, 1, qc[0, 1][:, P:2 * P])
         for r in range(4):
             for a in range(2):
                 product(banks[r // 2][:, r % 2, :], 0, 2, a, 1, r, False, r % 2 == 1 and a == 1)
 
-        def late_q(c, o, pool, **where):
-            round_q("scalar", c, 1, o, raw[c, o][:], pool, **where)
-            qc[c, o] = keep.tile([P, P], U32, name="qc%d%d" % (c, o), align_bytes=64)
-            quantise_q(c, 1, o, qc[c, o][:])
+        def late_q(c, pool, **where):
+            round_q("scalar", c, 1, 1, raw[c, 1][:], keep)
+            qc[c, 1] = pool.tile([P, P], U32, name="qc%d1" % c, align_bytes=64, **where)
+            quantise_q(c, 1, 1, qc[c, 1][:])
 
         def late_products(c, rows):
             late = [psum.tile([P, rows, P], F32, name="bank%d_%d" % (c, b)) for b in range(4 // rows)]
@@ -188,25 +210,28 @@ def tile_attend_plw_resid_topk_kernel(tc, qT, k_words, k_scales, c_words, c_scal
                                 (o, r % rows, a) == (0, 0, 0), (o, r % rows, a) == (1, rows - 1, 1))
             return late
 
-        late_q(2, 0, keep)
-        late_q(2, 1, keep)
-        z0 = subtract(banks[0], 0, 2, arena, "z0", offset=KW_AT + 2 * KIB, align_bytes=64)
+        round_pair(2, 0, (("scalar", raw[2, 0][:, :, 0:P]), ("vector", raw[2, 0][:, :, P:2 * P])))
+        qc[3, 0] = qc[2, 0][:, P:2 * P]
+        qc[2, 0] = qc[2, 0][:, 0:P]
+        late_q(2, keep)
+        z0 = subtract(banks[0], 0, 2, arena, "z0", offset=KW_AT + 7 * KIB // 2, align_bytes=64)
         bank_c = late_products(2, 4)
-        late_q(3, 0, keep)
         z1 = subtract(banks[1], 0, 2, keep, "z1")
-        late_q(3, 1, keep)
+        late_q(3, arena, offset=QC_AT)
         bank_d = late_products(3, 2)
-        y01 = arena.tile([P, 4, 2 * P], F32, name="y01", offset=KW_AT + 7 * KIB, align_bytes=64)
+        y01 = arena.tile([P, 4, 2 * P], F32, name="y01", offset=KW_AT + 7 * KIB + KIB // 2, align_bytes=64)
         weights(y01, z0, 0, 2, 0)
         weights(y01, z1, 0, 2, 2)
-        z2 = subtract(bank_c[0], 2, 1, arena, "z2", offset=KW_AT + 5 * KIB, align_bytes=64)
+        z2 = subtract(bank_c[0], 2, 1, arena, "z2", offset=KW_AT + 11 * KIB // 2, align_bytes=64)
         round_y(("scalar", "vector"), y01, 0)
         y2 = keep.tile([P, 4, P], F32, name="y2")
         weights(y2, z2, 2, 1, 0)
         z3 = [subtract(bank_d[b], 3, 1, keep, "z3_%d" % b) for b in range(2)]
         y3 = keep.tile([P, 4, P], F32, name="y3")
         for b in range(2):
-            weights(y3, z3[b], 3, 1, 2 * b)
+            nc.scalar.activation(y3[:, 2 * b:2 * b + 2, :], z3[b][:], ACT.Exp)
+        nc.sync.dma_start(out=out_rows[:, :, 3 * P:4 * P], in_=y3[:])
+        yc = arena.tile([P, NQ], U32, name="yc", offset=Q1_AT, align_bytes=64)
         quantise_y(0, 2)
         store_words(0)
         round_y(("vector",), y2, 2)

@@ -90,10 +90,10 @@ def tile_attend_plw_resid_topk_kernel(tc, qT, k_words, k_scales, c_words, c_scal
         def gather_words(a, window, pool, **where):
             g = pool.tile([P, N], U32, name="g%d" % a, **where)
             nc.vector.tensor_copy(g[:], window[:].bitcast(U32).indirect(offsets[:]))
-            return g[:].bitcast(U16).rearrange("p (s r h) -> p h s r", h=2, r=4)
+            return g[:].bitcast(U16).rearrange("p (x i r h) -> p h x r i", h=2, r=4, i=4)
 
         def part_words(a, pairs, lo, hi):
-            nc.vector.tensor_copy(halves[a][:, lo:hi].rearrange("p h r s -> p h s r"), pairs[:, lo:hi])
+            nc.vector.tensor_copy(halves[a][:, lo].rearrange("p r (x i) -> p x r i", i=4), pairs[:, lo])
 
         def interleave(engine, dst, src):
             dst = dst.rearrange("p (x i) t -> p x t i", i=4)

@@ -196,9 +196,9 @@ def tile_attend_plw_resid_topk_kernel(tc, qT, k_words, k_scales, c_words, c_scal
             for a in range(2):
                 product(banks[r // 2][:, r % 2, :], 0, 2, a, 1, r, False, r % 2 == 1 and a == 1)
 
-        def late_q(c, pool, **where):
-            round_q("scalar", c, 1, 1, raw[c, 1][:], keep)
-            qc[c, 1] = pool.tile([P, P], U32, name="qc%d1" % c, align_bytes=64, **where)
+        def late_q(c, engine, pool, **where):
+            round_q(engine, c, 1, 1, raw[c, 1][:], pool, **where)
+            qc[c, 1] = keep.tile([P, P], U32, name="qc%d1" % c, align_bytes=64)
             quantise_q(c, 1, 1, qc[c, 1][:])
 
         def late_products(c, rows):
@@ -213,13 +213,13 @@ def tile_attend_plw_resid_topk_kernel(tc, qT, k_words, k_scales, c_words, c_scal
         round_pair(2, 0, (("scalar", raw[2, 0][:, :, 0:P]), ("vector", raw[2, 0][:, :, P:2 * P])))
         qc[3, 0] = qc[2, 0][:, P:2 * P]
         qc[2, 0] = qc[2, 0][:, 0:P]
-        late_q(2, keep)
+        late_q(2, "scalar", keep)
         z0 = subtract(banks[0], 0, 2, arena, "z0", offset=KW_AT + 7 * KIB // 2, align_bytes=64)
         bank_c = late_products(2, 4)
         z1 = subtract(banks[1], 0, 2, keep, "z1")
-        late_q(3, arena, offset=QC_AT)
+        late_q(3, "vector", arena, offset=QC_AT)
         bank_d = late_products(3, 2)
-        y01 = arena.tile([P, 4, 2 * P], F32, name="y01", offset=KW_AT + 7 * KIB + KIB // 2, align_bytes=64)
+        y01 = keep.tile([P, 4, 2 * P], F32, name="y01")
         weights(y01, z0, 0, 2, 0)
         weights(y01, z1, 0, 2, 2)
         z2 = subtract(bank_c[0], 2, 1, arena, "z2", offset=KW_AT + 11 * KIB // 2, align_bytes=64)

@@ -61,10 +61,9 @@ def tile_attend_plw_resid_topk_kernel(tc, qT, k_words, k_scales, c_words, c_scal
         nc.sync.dma_start(out=kw[:], in_=k_words.rearrange("a p t b -> p (a t b)").bitcast(I32))
         load_q(arena, 0, 2, 0, offset=Q0_AT, align_bytes=64)
         nc.sync.dma_start(out=cw[:], in_=c_words.rearrange("a p t b -> p (a t b)").bitcast(I32))
-        load_q(arena, 0, 1, 1, offset=Q1_AT, align_bytes=64)
 
         planes = keep.tile([P, 2, 2, N], U8, name="planes", align_bytes=64)
-        nc.gpsimd.memset(planes[:].rearrange("p o a n -> p (o a n)").bitcast(I32), 0)
+        nc.vector.memset(planes[:].rearrange("p o a n -> p (o a n)").bitcast(I32), 0)
 
         gs = keep.tile([P, 2, N], U8, name="gs", align_bytes=64)
         for a in range(2):
@@ -77,7 +76,8 @@ def tile_attend_plw_resid_topk_kernel(tc, qT, k_words, k_scales, c_words, c_scal
                 out=planes[32 * u:32 * u + 4].rearrange("p o a n -> p o (a n)").bitcast(I32),
                 in_=dealt[96 + 8 * u:96 + 8 * u + 8].rearrange("p a r s -> p (a r s)").bitcast(I32),
             )
-        load_q(arena, 1, 1, 1, offset=WIN_AT + KIB, align_bytes=64)
+        for c in range(2):
+            load_q(arena, c, 1, 1, offset=WIN_AT + c * T, align_bytes=64)
 
         ls_bank = psum.tile([P, 4, P], F32, name="ls_bank")
         for j in range(4):
@@ -173,11 +173,6 @@ def tile_attend_plw_resid_topk_kernel(tc, qT, k_words, k_scales, c_words, c_scal
             nc.vector.quantize_mx(out=qc[0, 0][:, cols].bitcast(FP8X4), scales=qs[:, 0, cols],
                                   in_=qb[0, 0][:, cols, :].rearrange("p q t -> p (q t)"))
             part_words(0, pairs, c, c + 1)
-        spare = psum.tile([P, 2 * P], F32, name="spare")
-        for r in range(2):
-            nc.tensor.matmul_mx(
-                out=spare[:], lhsT=halves[0][:, 0, r, :].bitcast(FP4X4), lhsT_scale=qs[:, 0, 0:P],
-                rhs=qc[0, 0][:].bitcast(FP8X4), rhs_scale=qs[:, 0, 0:2 * P], start=True, stop=True)
         banks = [psum.tile([P, 2, 2 * P], F32, name="bank%d" % b) for b in range(2)]
         for r in range(4):
             product(banks[r // 2][:, r % 2, :], 0, 2, 0, 0, r, r % 2 == 0, False)
@@ -185,12 +180,12 @@ def tile_attend_plw_resid_topk_kernel(tc, qT, k_words, k_scales, c_words, c_scal
         qc[0, 1] = arena.tile([P, 2 * P], U32, name="qc01", offset=QC_AT, align_bytes=64)
         round_q("scalar", 0, 1, 1, raw[0, 1][:], keep)
         round_q("scalar", 1, 1, 1, raw[1, 1][:], keep)
-        quantise_q(0, 1, 1, qc[0, 1][:, 0:P])
         halves[1] = arena.tile([P, 2, 4, P], U16, name="h1", offset=Q1_AT, align_bytes=64)
         part_words(1, pairs, 0, 1)
         for r in range(4):
             product(banks[r // 2][:, r % 2, :], 0, 2, 1, 0, r, False, False)
         part_words(1, pairs, 1, 2)
+        quantise_q(0, 1, 1, qc[0, 1][:, 0:P])
         quantise_q(1, 1, 1, qc[0, 1][:, P:2 * P])
         for r in range(4):
             for a in range(2):

@@ -71,13 +71,13 @@ def tile_attend_plw_resid_topk_kernel(tc, qT, k_words, k_scales, c_words, c_scal
         dealt = keep.tile([P, 2, 4, P], U8, name="dealt", align_bytes=64)
         for a in range(2):
             nc.vector.tensor_copy(dealt[:, a], gs[:, a, :].rearrange("p (s r) -> p r s", r=4))
+        load_q(arena, 0, 1, 1, offset=WIN_AT, align_bytes=64)
         for u in range(4):
             nc.sync.dma_start(
                 out=planes[32 * u:32 * u + 4].rearrange("p o a n -> p o (a n)").bitcast(I32),
                 in_=dealt[96 + 8 * u:96 + 8 * u + 8].rearrange("p a r s -> p (a r s)").bitcast(I32),
             )
-        for c in range(2):
-            load_q(arena, c, 1, 1, offset=WIN_AT + c * T, align_bytes=64)
+        load_q(arena, 1, 1, 1, offset=WIN_AT + T, align_bytes=64)
 
         ls_bank = psum.tile([P, 4, P], F32, name="ls_bank")
         for j in range(4):
@@ -85,15 +85,16 @@ def tile_attend_plw_resid_topk_kernel(tc, qT, k_words, k_scales, c_words, c_scal
         ls_rows = keep.tile([P, NQ], F32, name="ls_rows")
         nc.scalar.copy(ls_rows[:].rearrange("p (n j) -> p n j", j=4), ls_bank[:].rearrange("p j n -> p n j"))
 
-        halves = {}
+        halves, gathered = {}, {}
 
         def gather_words(a, window, pool, **where):
             g = pool.tile([P, N], U32, name="g%d" % a, **where)
+            gathered[a] = g
             nc.vector.tensor_copy(g[:], window[:].bitcast(U32).indirect(offsets[:]))
             return g[:].bitcast(U16).rearrange("p (x i r h) -> p h x r i", h=2, r=4, i=4)
 
         def part_words(a, pairs, lo, hi):
-            nc.vector.tensor_copy(halves[a][:, lo].rearrange("p r (x i) -> p x r i", i=4), pairs[:, lo])
+            nc.vector.tensor_copy(halves[a, lo][:].rearrange("p r (x i) -> p x r i", i=4), pairs[:, lo])
 
         def interleave(engine, dst, src):
             dst = dst.rearrange("p (x i) t -> p x t i", i=4)
@@ -116,7 +117,7 @@ def tile_attend_plw_resid_topk_kernel(tc, qT, k_words, k_scales, c_words, c_scal
 
         def product(out, c, n, a, o, r, start, stop):
             nc.tensor.matmul_mx(
-                out=out, lhsT=halves[a][:, o, r, :].bitcast(FP4X4), lhsT_scale=planes[:, o, a, r * P:(r + 1) * P],
+                out=out, lhsT=halves[a, o][:, r, :].bitcast(FP4X4), lhsT_scale=planes[:, o, a, r * P:(r + 1) * P],
                 rhs=qc[c, o][:].bitcast(FP8X4), rhs_scale=qs[:, o, c * P:(c + n) * P], start=start, stop=stop)
 
         ys = keep.tile([P, NQ], U8, name="ys", align_bytes=64)
@@ -151,8 +152,7 @@ def tile_attend_plw_resid_topk_kernel(tc, qT, k_words, k_scales, c_words, c_scal
             pair = slice(c * P, (c + 2) * P)
             nc.sync.dma_start(out=out_words[:, pair], in_=yc[:, pair].bitcast(I32))
 
-        halves[0] = keep.tile([P, 2, 4, P], U16, name="h0", align_bytes=64)
-        pairs = gather_words(0, kw, keep)
+        pairs = gather_words(0, kw, keep, align_bytes=64)
         load_q(arena, 2, 2, 0, offset=KW_AT, align_bytes=64)
         for c in (2, 3):
             load_q(arena, c, 1, 1, offset=KW_AT + c * 2 * KIB, align_bytes=64)
@@ -172,15 +172,26 @@ def tile_attend_plw_resid_topk_kernel(tc, qT, k_words, k_scales, c_words, c_scal
             interleave("scalar", qb[0, 0][:, cols, :], raw[0, 0][:, :, cols])
             nc.vector.quantize_mx(out=qc[0, 0][:, cols].bitcast(FP8X4), scales=qs[:, 0, cols],
                                   in_=qb[0, 0][:, cols, :].rearrange("p q t -> p (q t)"))
-            part_words(0, pairs, c, c + 1)
+        idle = psum.tile([P, N], F32, name="idle")
+        for w in range(3):
+            nc.tensor.matmul_mx(
+                out=idle[:], lhsT=qc[0, 0][:, 0:P].bitcast(FP8X4), lhsT_scale=qs[:, 0, 0:P],
+                rhs=gathered[0][:, 0:N // 2].bitcast(FP4X4),
+                rhs_scale=dealt[:, 0].rearrange("p r s -> p (r s)"), start=True, stop=True)
+        for o in range(2):
+            halves[0, o] = arena.tile([P, 4, P], U16, name="h0%d" % o, offset=Q0_AT + (2 + o) * KIB, align_bytes=64)
+        coarse = pairs
+        part_words(0, coarse, 0, 1)
         banks = [psum.tile([P, 2, 2 * P], F32, name="bank%d" % b) for b in range(2)]
         for r in range(4):
             product(banks[r // 2][:, r % 2, :], 0, 2, 0, 0, r, r % 2 == 0, False)
         pairs = gather_words(1, cw, arena, offset=Q0_AT, align_bytes=64)
+        part_words(0, coarse, 1, 2)
         qc[0, 1] = arena.tile([P, 2 * P], U32, name="qc01", offset=QC_AT, align_bytes=64)
         round_q("scalar", 0, 1, 1, raw[0, 1][:], keep)
         round_q("scalar", 1, 1, 1, raw[1, 1][:], keep)
-        halves[1] = arena.tile([P, 2, 4, P], U16, name="h1", offset=Q1_AT, align_bytes=64)
+        for o in range(2):
+            halves[1, o] = arena.tile([P, 4, P], U16, name="h1%d" % o, offset=Q1_AT + o * KIB, align_bytes=64)
         part_words(1, pairs, 0, 1)
         for r in range(4):
             product(banks[r // 2][:, r % 2, :], 0, 2, 1, 0, r, False, False)
@@ -212,13 +223,15 @@ def tile_attend_plw_resid_topk_kernel(tc, qT, k_words, k_scales, c_words, c_scal
         z0 = subtract(banks[0], 0, 2, arena, "z0", offset=KW_AT + 7 * KIB // 2, align_bytes=64)
         bank_c = late_products(2, 4)
         z1 = subtract(banks[1], 0, 2, keep, "z1")
-        late_q(3, "vector", arena, offset=QC_AT)
+        round_q("scalar", 3, 1, 1, raw[3, 1][:], keep)
+        qc[3, 1] = arena.tile([P, P], U32, name="qc31", offset=QC_AT, align_bytes=64)
+        quantise_q(3, 1, 1, qc[3, 1][:])
         bank_d = late_products(3, 2)
         y01 = keep.tile([P, 4, 2 * P], F32, name="y01")
         weights(y01, z0, 0, 2, 0)
         weights(y01, z1, 0, 2, 2)
         z2 = subtract(bank_c[0], 2, 1, arena, "z2", offset=KW_AT + 11 * KIB // 2, align_bytes=64)
-        round_y(("scalar", "vector"), y01, 0)
+        round_y(("vector",), y01[:, :, P:2 * P], 1)
         y2 = keep.tile([P, 4, P], F32, name="y2")
         weights(y2, z2, 2, 1, 0)
         z3 = [subtract(bank_d[b], 3, 1, keep, "z3_%d" % b) for b in range(2)]
@@ -226,14 +239,17 @@ def tile_attend_plw_resid_topk_kernel(tc, qT, k_words, k_scales, c_words, c_scal
         for b in range(2):
             nc.scalar.activation(y3[:, 2 * b:2 * b + 2, :], z3[b][:], ACT.Exp)
         nc.sync.dma_start(out=out_rows[:, :, 3 * P:4 * P], in_=y3[:])
-        yc = arena.tile([P, NQ], U32, name="yc", offset=Q1_AT, align_bytes=64)
-        quantise_y(0, 2)
-        store_words(0)
+        yb[0] = arena.tile([P, P, 4], BF16, name="yb0", offset=Q1_AT + KIB, align_bytes=64)
+        interleave("scalar", yb[0][:], y01[:, :, 0:P])
+        yc = arena.tile([P, NQ], U32, name="yc", offset=Q0_AT + 2 * KIB, align_bytes=64)
         round_y(("vector",), y2, 2)
+        quantise_y(1, 1)
         round_y(("vector",), y3, 3)
         quantise_y(2, 1)
         quantise_y(3, 1)
         store_words(2)
+        quantise_y(0, 1)
+        store_words(0)
         for u in range(4):
             queue = nc.sync if u % 2 else nc.scalar
             queue.dma_start(out=out_2[0, 4 * u:4 * u + 4, :].bitcast(I32),

@@ -72,7 +72,7 @@ def tile_attend_plw_resid_topk_kernel(tc, qT, k_words, k_scales, c_words, c_scal
         for a in range(2):
             nc.vector.tensor_copy(dealt[:, a], gs[:, a, :].rearrange("p (s r) -> p r s", r=4))
         load_q(arena, 0, 1, 1, offset=WIN_AT, align_bytes=64)
-        for u in range(4):
+        for u in (0, 2, 1, 3):
             nc.sync.dma_start(
                 out=planes[32 * u:32 * u + 4].rearrange("p o a n -> p o (a n)").bitcast(I32),
                 in_=dealt[96 + 8 * u:96 + 8 * u + 8].rearrange("p a r s -> p (a r s)").bitcast(I32),

@@ -172,10 +172,10 @@ def tile_attend_plw_resid_topk_kernel(tc, qT, k_words, k_scales, c_words, c_scal
             interleave("scalar", qb[0, 0][:, cols, :], raw[0, 0][:, :, cols])
             nc.vector.quantize_mx(out=qc[0, 0][:, cols].bitcast(FP8X4), scales=qs[:, 0, cols],
                                   in_=qb[0, 0][:, cols, :].rearrange("p q t -> p (q t)"))
-        idle = psum.tile([P, N], F32, name="idle")
+        idle = ls_bank[:].rearrange("p j n -> p (j n)")
         for w in range(3):
             nc.tensor.matmul_mx(
-                out=idle[:], lhsT=qc[0, 0][:, 0:P].bitcast(FP8X4), lhsT_scale=qs[:, 0, 0:P],
+                out=idle, lhsT=qc[0, 0][:, 0:P].bitcast(FP8X4), lhsT_scale=qs[:, 0, 0:P],
                 rhs=gathered[0][:, 0:N // 2].bitcast(FP4X4),
                 rhs_scale=dealt[:, 0].rearrange("p r s -> p (r s)"), start=True, stop=True)
         for o in range(2):
@@ -226,7 +226,7 @@ def tile_attend_plw_resid_topk_kernel(tc, qT, k_words, k_scales, c_words, c_scal
         round_q("scalar", 3, 1, 1, raw[3, 1][:], keep)
         qc[3, 1] = arena.tile([P, P], U32, name="qc31", offset=QC_AT, align_bytes=64)
         quantise_q(3, 1, 1, qc[3, 1][:])
-        bank_d = late_products(3, 2)
+        bank_d = late_products(3, 1)
         y01 = keep.tile([P, 4, 2 * P], F32, name="y01")
         weights(y01, z0, 0, 2, 0)
         weights(y01, z1, 0, 2, 2)
@@ -234,22 +234,25 @@ def tile_attend_plw_resid_topk_kernel(tc, qT, k_words, k_scales, c_words, c_scal
         round_y(("vector",), y01[:, :, P:2 * P], 1)
         y2 = keep.tile([P, 4, P], F32, name="y2")
         weights(y2, z2, 2, 1, 0)
-        z3 = [subtract(bank_d[b], 3, 1, keep, "z3_%d" % b) for b in range(2)]
+        z3 = keep.tile([P, 4, P], F32, name="z3")
         y3 = keep.tile([P, 4, P], F32, name="y3")
-        for b in range(2):
-            nc.scalar.activation(y3[:, 2 * b:2 * b + 2, :], z3[b][:], ACT.Exp)
+        for b in range(4):
+            nc.vector.tensor_tensor(z3[:, b, :], bank_d[b][:, 0, :], ls_rows[:, 3 * P:4 * P], mybir.AluOpType.subtract)
+            nc.scalar.activation(y3[:, b, :], z3[:, b, :], ACT.Exp)
         nc.sync.dma_start(out=out_rows[:, :, 3 * P:4 * P], in_=y3[:])
+        yb[3] = keep.tile([P, P, 4], BF16, name="yb3", align_bytes=64)
+        nc.scalar.activation(yb[3][:].rearrange("p (x i) t -> p x t i", i=4),
+                             z3[:].rearrange("p t (x i) -> p x t i", i=4), ACT.Exp)
         yb[0] = arena.tile([P, P, 4], BF16, name="yb0", offset=Q1_AT + KIB, align_bytes=64)
-        interleave("scalar", yb[0][:], y01[:, :, 0:P])
+        interleave("vector", yb[0][:], y01[:, :, 0:P])
         yc = arena.tile([P, NQ], U32, name="yc", offset=Q0_AT + 2 * KIB, align_bytes=64)
         round_y(("vector",), y2, 2)
+        quantise_y(0, 1)
         quantise_y(1, 1)
-        round_y(("vector",), y3, 3)
+        store_words(0)
         quantise_y(2, 1)
         quantise_y(3, 1)
         store_words(2)
-        quantise_y(0, 1)
-        store_words(0)
         for u in range(4):
             queue = nc.sync if u % 2 else nc.scalar
             queue.dma_start(out=out_2[0, 4 * u:4 * u + 4, :].bitcast(I32),

from contextlib import ExitStack

import concourse.mybir as mybir
from concourse.masks import make_identity

F32 = mybir.dt.float32
BF16 = mybir.dt.bfloat16
I32 = mybir.dt.int32
U32 = mybir.dt.uint32
U16 = mybir.dt.uint16
U8 = mybir.dt.uint8
FP8X4 = mybir.dt.float8_e4m3fn_x4
FP4X4 = mybir.dt.float4_e2m1fn_x4
ACT = mybir.ActivationFunctionType

P = 128
N, T, D, NQ = 512, 2048, 1024, 512
CH = NQ // P
FLOPS = 2 * 2 * N * D * NQ
KIB = 1024


def tile_attend_plw_resid_topk_kernel(tc, qT, k_words, k_scales, c_words, c_scales, ls, offs, out_0, out_1, out_2):
    nc = tc.nc
    with ExitStack() as ctx:
        keep = ctx.enter_context(tc.tile_pool(name="keep", bufs=1))
        arena = ctx.enter_context(tc.tile_pool(name="arena", bufs=1))
        psum = ctx.enter_context(tc.psum_pool(name="psum", bufs=1))

        offsets = keep.tile([P, N // 16], U16, name="offsets")
        nc.sync.dma_start(offsets[:], offs)

        KW_AT = 0
        Q0_AT = 12 * KIB
        LS_AT = 16 * KIB
        Q1_AT = 18 * KIB
        QC_AT = 20 * KIB
        WIN_AT = 8 * KIB

        windows = []
        for a, scales in enumerate((k_scales, c_scales)):
            window = arena.tile([P, T // 4], I32, name="window%d" % a, offset=WIN_AT + a * T, align_bytes=64)
            (nc.scalar if a else nc.sync).dma_start(out=window[96:P, :], in_=scales.rearrange("o f t -> f o t").bitcast(I32))
            nc.vector.memset(window[0:96, :], 0)
            windows.append(window)
        ls_cols = arena.tile([P, 4], F32, name="ls_cols", offset=LS_AT, align_bytes=64)
        nc.scalar.dma_start(out=ls_cols[:], in_=ls.rearrange("a b (p j) -> p (a b j)", j=4))
        ident = keep.tile([P, P], F32, name="ident")
        make_identity(nc, ident[:])

        raw = {}

        def load_q(pool, c, n, o, **where):
            piece = pool.tile([P, 4, n * P], F32, name="raw%d%d" % (c, o), **where)
            rows = qT[0, o * 512:(o + 1) * 512, c * P:(c + n) * P]
            nc.sync.dma_start(out=piece[:], in_=rows.rearrange("(p j) q -> p j q", j=4))
            raw[c, o] = piece

        kw = arena.tile([P, T], I32, name="kw", offset=KW_AT, align_bytes=64)
        cw = keep.tile([P, T], I32, name="cw")
        nc.sync.dma_start(out=kw[:], in_=k_words.rearrange("a p t b -> p (a t b)").bitcast(I32))
        load_q(arena, 0, 2, 0, offset=Q0_AT, align_bytes=64)
        nc.sync.dma_start(out=cw[:], in_=c_words.rearrange("a p t b -> p (a t b)").bitcast(I32))

        planes = keep.tile([P, 2, 2, N], U8, name="planes", align_bytes=64)
        nc.vector.memset(planes[:].rearrange("p o a n -> p (o a n)").bitcast(I32), 0)

        gs = keep.tile([P, 2, N], U8, name="gs", align_bytes=64)
        for a in range(2):
            nc.vector.tensor_copy(gs[:, a, :], windows[a][:].bitcast(U8).indirect(offsets[:]))
        dealt = keep.tile([P, 2, 4, P], U8, name="dealt", align_bytes=64)
        for a in range(2):
            nc.vector.tensor_copy(dealt[:, a], gs[:, a, :].rearrange("p (s r) -> p r s", r=4))
        load_q(arena, 0, 1, 1, offset=WIN_AT, align_bytes=64)
        for u in (0, 2, 1, 3):
            nc.sync.dma_start(
                out=planes[32 * u:32 * u + 4].rearrange("p o a n -> p o (a n)").bitcast(I32),
                in_=dealt[96 + 8 * u:96 + 8 * u + 8].rearrange("p a r s -> p (a r s)").bitcast(I32),
            )
        load_q(arena, 1, 1, 1, offset=WIN_AT + T, align_bytes=64)

        ls_bank = psum.tile([P, 4, P], F32, name="ls_bank")
        for j in range(4):
            nc.tensor.transpose(ls_bank[:, j, :], ls_cols[:, j:j + 1].to_broadcast([P, P]), ident[:])
        ls_rows = keep.tile([P, NQ], F32, name="ls_rows")
        nc.scalar.copy(ls_rows[:].rearrange("p (n j) -> p n j", j=4), ls_bank[:].rearrange("p j n -> p n j"))

        halves, gathered = {}, {}

        def gather_words(a, window, pool, **where):
            g = pool.tile([P, N], U32, name="g%d" % a, **where)
            gathered[a] = g
            nc.vector.tensor_copy(g[:], window[:].bitcast(U32).indirect(offsets[:]))
            return g[:].bitcast(U16).rearrange("p (x i r h) -> p h x r i", h=2, r=4, i=4)

        def part_words(a, pairs, lo, hi):
            nc.vector.tensor_copy(halves[a, lo][:].rearrange("p r (x i) -> p x r i", i=4), pairs[:, lo])

        def interleave(engine, dst, src):
            dst = dst.rearrange("p (x i) t -> p x t i", i=4)
            src = src.rearrange("p t (x i) -> p x t i", i=4)
            if engine == "scalar":
                nc.scalar.activation(dst, src, ACT.Copy)
            else:
                nc.vector.tensor_copy(dst, src)

        qb, qc = {}, {}
        qs = keep.tile([P, 2, NQ], U8, name="qs", align_bytes=64)

        def round_q(engine, c, n, o, src, pool, **where):
            qb[c, o] = pool.tile([P, n * P, 4], BF16, name="qb%d%d" % (c, o), align_bytes=64, **where)
            interleave(engine, qb[c, o][:], src)

        def quantise_q(c, n, o, codes):
            nc.vector.quantize_mx(out=codes.bitcast(FP8X4), scales=qs[:, o, c * P:(c + n) * P],
                                  in_=qb[c, o][:].rearrange("p q t -> p (q t)"))

        def product(out, c, n, a, o, r, start, stop):
            nc.tensor.matmul_mx(
                out=out, lhsT=halves[a, o][:, r, :].bitcast(FP4X4), lhsT_scale=planes[:, o, a, r * P:(r + 1) * P],
                rhs=qc[c, o][:].bitcast(FP8X4), rhs_scale=qs[:, o, c * P:(c + n) * P], start=start, stop=stop)

        ys = keep.tile([P, NQ], U8, name="ys", align_bytes=64)
        out_rows = out_0.rearrange("(s r) q -> s r q", r=4)
        out_words = out_1.rearrange("a p q t -> p (a q t)").bitcast(I32)

        def subtract(bank, c, n, pool, name, **where):
            rows = bank.shape[1]
            z = pool.tile([P, rows, n * P], F32, name=name, **where)
            spread = ls_rows[:, c * P:(c + n) * P].unsqueeze(1).to_broadcast([P, rows, n * P])
            nc.vector.tensor_tensor(z[:], bank[:], spread, mybir.AluOpType.subtract)
            return z

        def weights(y, z, c, n, r0):
            rows = slice(r0, r0 + z.shape[1])
            nc.scalar.activation(y[:, rows, :], z[:], ACT.Exp)
            nc.sync.dma_start(out=out_rows[:, rows, c * P:(c + n) * P], in_=y[:, rows, :])

        yb = {}

        def round_y(engines, y, c):
            yb[c] = keep.tile([P, len(engines) * P, 4], BF16, name="yb%d" % c, align_bytes=64)
            for i, engine in enumerate(engines):
                interleave(engine, yb[c][:, i * P:(i + 1) * P, :], y[:, :, i * P:(i + 1) * P])

        def quantise_y(c, n):
            cols = slice(c * P, (c + n) * P)
            nc.vector.quantize_mx(out=yc[:, cols].bitcast(FP8X4), scales=ys[:, cols],
                                  in_=yb[c][:].rearrange("p q t -> p (q t)"))

        def store_words(c):
            pair = slice(c * P, (c + 2) * P)
            nc.sync.dma_start(out=out_words[:, pair], in_=yc[:, pair].bitcast(I32))

        pairs = gather_words(0, kw, keep, align_bytes=64)
        load_q(arena, 2, 2, 0, offset=KW_AT, align_bytes=64)
        for c in (2, 3):
            load_q(arena, c, 1, 1, offset=KW_AT + c * 2 * KIB, align_bytes=64)

        def round_pair(c, o, parts):
            qb[c, o] = keep.tile([P, 2 * P, 4], BF16, name="qb%d%d" % (c, o), align_bytes=64)
            for i, (engine, src) in enumerate(parts):
                width = src.shape[2]
                interleave(engine, qb[c, o][:, i * width:(i + 1) * width, :], src)
            qc[c, o] = keep.tile([P, 2 * P], U32, name="qc%d%d" % (c, o), align_bytes=64)
            quantise_q(c, 2, o, qc[c, o][:])

        qb[0, 0] = arena.tile([P, 2 * P, 4], BF16, name="qb00", offset=LS_AT, align_bytes=64)
        qc[0, 0] = keep.tile([P, 2 * P], U32, name="qc00", align_bytes=64)
        for c in range(2):
            cols = slice(c * P, (c + 1) * P)
            interleave("scalar", qb[0, 0][:, cols, :], raw[0, 0][:, :, cols])
            nc.vector.quantize_mx(out=qc[0, 0][:, cols].bitcast(FP8X4), scales=qs[:, 0, cols],
                                  in_=qb[0, 0][:, cols, :].rearrange("p q t -> p (q t)"))
        idle = ls_bank[:].rearrange("p j n -> p (j n)")
        for w in range(3):
            nc.tensor.matmul_mx(
                out=idle, lhsT=qc[0, 0][:, 0:P].bitcast(FP8X4), lhsT_scale=qs[:, 0, 0:P],
                rhs=gathered[0][:, 0:N // 2].bitcast(FP4X4),
                rhs_scale=dealt[:, 0].rearrange("p r s -> p (r s)"), start=True, stop=True)
        for o in range(2):
            halves[0, o] = arena.tile([P, 4, P], U16, name="h0%d" % o, offset=Q0_AT + (2 + o) * KIB, align_bytes=64)
        coarse = pairs
        part_words(0, coarse, 0, 1)
        banks = [psum.tile([P, 2, 2 * P], F32, name="bank%d" % b) for b in range(2)]
        for r in range(4):
            product(banks[r // 2][:, r % 2, :], 0, 2, 0, 0, r, r % 2 == 0, False)
        pairs = gather_words(1, cw, arena, offset=Q0_AT, align_bytes=64)
        part_words(0, coarse, 1, 2)
        qc[0, 1] = arena.tile([P, 2 * P], U32, name="qc01", offset=QC_AT, align_bytes=64)
        round_q("scalar", 0, 1, 1, raw[0, 1][:], keep)
        round_q("scalar", 1, 1, 1, raw[1, 1][:], keep)
        for o in range(2):
            halves[1, o] = arena.tile([P, 4, P], U16, name="h1%d" % o, offset=Q1_AT + o * KIB, align_bytes=64)
        part_words(1, pairs, 0, 1)
        for r in range(4):
            product(banks[r // 2][:, r % 2, :], 0, 2, 1, 0, r, False, False)
        part_words(1, pairs, 1, 2)
        quantise_q(0, 1, 1, qc[0, 1][:, 0:P])
        quantise_q(1, 1, 1, qc[0, 1][:, P:2 * P])
        for r in range(4):
            for a in range(2):
                product(banks[r // 2][:, r % 2, :], 0, 2, a, 1, r, False, r % 2 == 1 and a == 1)

        def late_q(c, engine, pool, **where):
            round_q(engine, c, 1, 1, raw[c, 1][:], pool, **where)
            qc[c, 1] = keep.tile([P, P], U32, name="qc%d1" % c, align_bytes=64)
            quantise_q(c, 1, 1, qc[c, 1][:])

        def late_products(c, rows):
            late = [psum.tile([P, rows, P], F32, name="bank%d_%d" % (c, b)) for b in range(4 // rows)]
            for o in range(2):
                for r in range(4):
                    for a in range(2):
                        product(late[r // rows][:, r % rows, :], c, 1, a, o, r,
                                (o, r % rows, a) == (0, 0, 0), (o, r % rows, a) == (1, rows - 1, 1))
            return late

        round_pair(2, 0, (("scalar", raw[2, 0][:, :, 0:P]), ("vector", raw[2, 0][:, :, P:2 * P])))
        qc[3, 0] = qc[2, 0][:, P:2 * P]
        qc[2, 0] = qc[2, 0][:, 0:P]
        late_q(2, "scalar", keep)
        z0 = subtract(banks[0], 0, 2, arena, "z0", offset=KW_AT + 7 * KIB // 2, align_bytes=64)
        bank_c = late_products(2, 4)
        z1 = subtract(banks[1], 0, 2, keep, "z1")
        round_q("scalar", 3, 1, 1, raw[3, 1][:], keep)
        qc[3, 1] = arena.tile([P, P], U32, name="qc31", offset=QC_AT, align_bytes=64)
        quantise_q(3, 1, 1, qc[3, 1][:])
        bank_d = late_products(3, 1)
        y01 = keep.tile([P, 4, 2 * P], F32, name="y01")
        weights(y01, z0, 0, 2, 0)
        weights(y01, z1, 0, 2, 2)
        z2 = subtract(bank_c[0], 2, 1, arena, "z2", offset=KW_AT + 11 * KIB // 2, align_bytes=64)
        round_y(("vector",), y01[:, :, P:2 * P], 1)
        y2 = keep.tile([P, 4, P], F32, name="y2")
        weights(y2, z2, 2, 1, 0)
        z3 = keep.tile([P, 4, P], F32, name="z3")
        y3 = keep.tile([P, 4, P], F32, name="y3")
        for b in range(4):
            nc.vector.tensor_tensor(z3[:, b, :], bank_d[b][:, 0, :], ls_rows[:, 3 * P:4 * P], mybir.AluOpType.subtract)
            nc.scalar.activation(y3[:, b, :], z3[:, b, :], ACT.Exp)
        nc.sync.dma_start(out=out_rows[:, :, 3 * P:4 * P], in_=y3[:])
        yb[3] = keep.tile([P, P, 4], BF16, name="yb3", align_bytes=64)
        nc.scalar.activation(yb[3][:].rearrange("p (x i) t -> p x t i", i=4),
                             z3[:].rearrange("p t (x i) -> p x t i", i=4), ACT.Exp)
        yb[0] = arena.tile([P, P, 4], BF16, name="yb0", offset=Q1_AT + KIB, align_bytes=64)
        interleave("vector", yb[0][:], y01[:, :, 0:P])
        yc = arena.tile([P, NQ], U32, name="yc", offset=Q0_AT + 2 * KIB, align_bytes=64)
        round_y(("vector",), y2, 2)
        quantise_y(0, 1)
        quantise_y(1, 1)
        store_words(0)
        quantise_y(2, 1)
        quantise_y(3, 1)
        store_words(2)
        for u in range(4):
            queue = nc.sync if u % 2 else nc.scalar
            queue.dma_start(out=out_2[0, 4 * u:4 * u + 4, :].bitcast(I32),
                            in_=ys[32 * u:32 * u + 4, :].bitcast(I32))
